import numpy as np
import ml_dtypes


def mxq(x, axis, fmt="e4m3"):
    dtype, down = {"e4m3": (ml_dtypes.float8_e4m3fn, 7), "e5m2": (ml_dtypes.float8_e5m2, 14)}[fmt]
    v = np.moveaxis(np.asarray(x, np.float32).astype(ml_dtypes.bfloat16).astype(np.float64), axis, -1)
    blocks = v.reshape(v.shape[:-1] + (-1, 32))
    amax = np.abs(blocks).max(-1, keepdims=True)
    byte = np.maximum(np.where(amax > 0, np.frexp(amax)[1] - 1 + 127, 0) - down, 1)
    scale = np.exp2(byte - 127.0)
    codes = (blocks / scale).astype(np.float32).astype(dtype).astype(np.float64)
    return np.moveaxis((codes * scale).reshape(v.shape), -1, axis)


WIDE = False


def mx_kscale(k):
    if not WIDE:
        return np.ones(k)
    levels = np.array([10, -10, 5, -5, 0])
    if k % 512:
        return np.exp2(np.random.permutation(np.resize(levels, k // 32))).repeat(32)
    a = np.empty((k // 512, 16))
    for p in range(k // 512):
        a[p, :8] = np.random.permutation(np.resize(levels, 8))
        for g in range(8):
            far = levels[np.abs(levels - a[p, g]) >= 10]
            a[p, g + 8] = far[np.random.randint(len(far))]
    return np.exp2(a.ravel()).repeat(32)


def f64(x):
    return np.asarray(x).astype(np.float64)


def striped(idx):
    return np.tile(idx.reshape(-1, 16).T, (8, 1)).astype(np.uint16)


def unstriped(offs):
    return offs[:16].T.reshape(-1).astype(np.int64)


E2M1 = np.array([0.0, 0.5, 1.0, 1.5, 2.0, 3.0, 4.0, 6.0, -0.0, -0.5, -1.0, -1.5, -2.0, -3.0, -4.0, -6.0])


def pack_weight(w, fmt):
    k, n = w.shape
    w = f64(np.asarray(w, np.float32).astype(ml_dtypes.bfloat16)).reshape(k // 32, 32, n)
    amax = np.abs(w).max(1)
    if fmt == "e4m3":
        byte = np.frexp(amax)[1] - 1 + 127 - 7
    else:
        mant, ex = np.frexp(amax / 6.0)
        byte = np.where(mant > 0.5, ex, ex - 1) + 127
    byte = np.clip(np.where(amax > 0, byte, 1), 1, 254)
    scaled = (w * np.exp2(127.0 - byte)[:, None, :]).reshape(k, n).astype(np.float32)
    by_word = np.ascontiguousarray(scaled.reshape(k // 512, 128, 4, n).transpose(0, 1, 3, 2))
    if fmt == "e4m3":
        words = by_word.astype(ml_dtypes.float8_e4m3fn).view(np.uint8)
    else:
        c = by_word.astype(ml_dtypes.float4_e2m1fn).view(np.uint8) & 0xF
        words = (c[..., 0::2] | (c[..., 1::2] << 4)).reshape(k // 512, 128, 2 * n)
    return np.ascontiguousarray(words), np.ascontiguousarray(byte.astype(np.uint8).reshape(k // 512, 16, n))


def unpack_weight(words, scales, fmt):
    g, _, n = scales.shape
    words = np.ascontiguousarray(words).reshape(g, 128, n, -1)
    if fmt == "e4m3":
        vals = words.view(ml_dtypes.float8_e4m3fn).astype(np.float64)
    else:
        nib = np.empty((g, 128, n, 4), np.uint8)
        nib[..., 0::2] = words & 0xF
        nib[..., 1::2] = words >> 4
        vals = E2M1[nib]
    vals = vals * np.repeat(np.exp2(scales.astype(np.float64) - 127.0), 8, axis=1)[..., None]
    return vals.transpose(0, 1, 3, 2).reshape(g * 512, n)


def gelu(v):
    return 0.5 * v * (1.0 + np.tanh(np.sqrt(2.0 / np.pi) * (v + 0.044715 * v**3)))


def striped8(idx):
    return np.concatenate([v.reshape(-1, 16).T for v in idx]).astype(np.uint16)


def unstriped8(offs):
    return np.stack([offs[16 * g:16 * g + 16].T.reshape(-1) for g in range(8)]).astype(np.int64)


def runs(v, idx8):
    k = np.arange(v.shape[0])
    return v[k[:, None], idx8[k % 512 // 64]]


def often(T, S):
    return np.random.permutation(T)[(T * np.random.uniform(0, 1, S) ** 4).astype(np.int64)]


K, H, T, S = 1536, 1024, 2048, 512

def setup_inputs():
    n = np.random.standard_normal
    s = mx_kscale(K)[:, None]
    u = mx_kscale(H)[:, None]
    tab_words, tab_scales = pack_weight(n((K, T)) * s, "e4m3")
    w4_words, w4_scales = pack_weight(1.5 * n((K, H)) / np.sqrt(K) / s, "e2m1")
    w8_words, w8_scales = pack_weight(0.3 * n((K, H)) / np.sqrt(K) / s / u.T, "e4m3")
    return {
        "tab_words": tab_words, "tab_scales": tab_scales,
        "offs": striped8(np.stack([often(T, S) for _ in range(8)])),
        "w4_words": w4_words, "w4_scales": w4_scales,
        "w8_words": w8_words, "w8_scales": w8_scales,
        "docs": (n((K, S)) / np.sqrt(K) / s).astype(np.float32),
        "b1": (0.5 * n(H)).astype(np.float32),
        "gain": (0.3 * np.exp(0.3 * n(H)) * u[:, 0]).astype(np.float32),
        "b2": (0.1 * n(H) / u[:, 0]).astype(np.float32),
    }

def reference(tab_words, tab_scales, offs, w4_words, w4_scales, w8_words, w8_scales, docs, b1, gain, b2):
    v = runs(unpack_weight(tab_words, tab_scales, "e4m3"), unstriped8(offs))
    w4 = unpack_weight(w4_words, w4_scales, "e2m1")
    w8 = unpack_weight(w8_words, w8_scales, "e4m3")
    a = (w4.T @ v) + f64(b1)[:, None]
    h = f64(gain)[:, None] / (1.0 + np.exp(-a))
    b = (w8.T @ v) + f64(b2)[:, None]
    d = mxq(f64(docs), 0, "e4m3").T @ v
    e = mxq(h, 0, "e4m3").T @ mxq(b, 0, "e4m3")
    return e * d

@@ -1,0 +1,257 @@
+from contextlib import ExitStack
+
+import concourse.mybir as mybir
+from concourse.masks import make_identity
+
+K, H, T, S = 1536, 1024, 2048, 512
+FLOPS = 2 * K * H * S * 2 + 2 * K * S * S + 2 * H * S * S
+
+F32 = mybir.dt.float32
+BF16 = mybir.dt.bfloat16
+I32 = mybir.dt.int32
+U32 = mybir.dt.uint32
+U16 = mybir.dt.uint16
+U8 = mybir.dt.uint8
+FP8X4 = mybir.dt.float8_e4m3fn_x4
+FP4X4 = mybir.dt.float4_e2m1fn_x4
+MULT = mybir.AluOpType.mult
+ADD = mybir.AluOpType.add
+SIGMOID = mybir.ActivationFunctionType.Sigmoid
+
+P = 128
+PACK = 4
+KP = K // (P * PACK)
+RP = H // (P * PACK)
+CT = H // P
+GROUPS = 16
+RUN = 8
+MT = S // P
+
+
+def tile_list_repository_matrix_kernel(
+    tc, tab_words, tab_scales, offs, w4_words, w4_scales, w8_words, w8_scales, docs, b1, gain, b2, out
+):
+    nc = tc.nc
+    with ExitStack() as ctx:
+        keep = ctx.enter_context(tc.tile_pool(name="keep", bufs=1))
+        psum = ctx.enter_context(tc.psum_pool(name="psum", bufs=1))
+
+        def sb(shape, dtype, name, tag=None):
+            return keep.tile(shape, dtype, name=name, tag=tag or name, align_bytes=64)
+
+        def bank(n, shape, name):
+            return psum.tile(shape, F32, name=name, tag="bank%d" % n)
+
+        offsets = keep.tile([P, S // 16], U16, name="offsets")
+        nc.sync.dma_start(offsets[:], offs)
+
+        win_tags = ["slot1", "slot2", "win2"]
+        wins = []
+        ws_raw = sb([P, KP, H // 4], I32, "ws_raw")
+
+        def load_w_scales(queue, scales):
+            for d in range(4):
+                queue.dma_start(
+                    ws_raw[32 * d : 32 * d + 4, :, :],
+                    scales.bitcast(I32)[:, 4 * d : 4 * d + 4, :].rearrange("a r n -> r a n"),
+                )
+
+        for a in range(KP):
+            win = sb([P, T], U8, "win%d" % a, win_tags[a])
+            nc.vector.memset(win[:].bitcast(I32), 0)
+            nc.scalar.dma_start(win[0:P:8, :].bitcast(I32), tab_scales[a].bitcast(I32))
+            wins.append(win)
+            if a == 0:
+                nc.vector.memset(ws_raw[:], 0)
+                load_w_scales(nc.gpsimd, w4_scales)
+
+        w4_raw = sb([P, KP, H // 2], I32, "w4_raw")
+        nc.sync.dma_start(w4_raw[:], w4_words.bitcast(I32).rearrange("a p n -> p a n"))
+
+        def load_tab(a, tag):
+            tab = sb([P, T], I32, "tab%d" % a, tag)
+            nc.sync.dma_start(tab[:], tab_words[a].rearrange("p t i -> p (t i)").bitcast(I32))
+            return tab
+
+        tab0 = load_tab(0, "slot0")
+
+        v_plane = sb([P, KP * S], U8, "v_plane")
+        nc.vector.memset(v_plane[:].bitcast(I32), 0)
+
+        ident = sb([P, P], F32, "ident")
+        make_identity(nc, ident[:])
+        rows = sb([P, P], F32, "rows")
+        nc.vector.memset(rows[:], 0.0)
+        for n, vec in enumerate((b1, gain, b2)):
+            nc.gpsimd.dma_start(
+                rows[CT * n : CT * (n + 1), :].rearrange("c (g i) -> c g i", i=RUN),
+                vec.rearrange("(g c i) -> c g i", c=CT, i=RUN),
+            )
+
+        picked = sb([P, KP * S], U8, "picked")
+        tabs = [tab0]
+        for a in range(KP):
+            nc.vector.tensor_copy(picked[:, a * S : (a + 1) * S], wins[a][:].indirect(offsets[:]))
+            if a + 1 < KP:
+                tabs.append(load_tab(a + 1, win_tags[a]))
+        for r in range(4):
+            nc.scalar.dma_start(v_plane[r:P:32, :].bitcast(I32), picked[8 * r : P : 32, :].bitcast(I32))
+
+        def permute(dst, src, words):
+            nc.vector.tensor_copy(
+                dst.rearrange("p (c g w) -> p c g w", c=CT, w=words),
+                src.rearrange("p (g c w) -> p c g w", c=CT, w=words),
+            )
+
+        def gather_words(a):
+            v = sb([P, S], I32, "v%d" % a)
+            nc.vector.tensor_copy(v[:].bitcast(U32), tabs[a][:].bitcast(U32).indirect(offsets[:]))
+            return v
+
+        vs = [gather_words(0)]
+        w4 = []
+        w4s = []
+        for a in range(KP):
+            ws = sb([P, H // 4], I32, "w4s_%d" % a)
+            permute(ws[:], ws_raw[:, a, :], 2)
+            w = sb([P, H // 2], I32, "w4_%d" % a)
+            permute(w[:], w4_raw[:, a, :], 4)
+            w4.append(w)
+            w4s.append(ws)
+
+        w8_all = w8_words.rearrange("a p n i -> p a (n i)").bitcast(I32)
+        w8_lo = sb([P, 2, H], I32, "w8_lo", "slot0")
+        nc.sync.dma_start(w8_lo[:], w8_all[:, 0:2, :])
+        load_w_scales(nc.scalar, w8_scales)
+        vs.append(gather_words(1))
+        w8_hi = sb([P, 1, H], I32, "w8_hi", "slot1")
+        nc.sync.dma_start(w8_hi[:], w8_all[:, 2:3, :])
+        vs.append(gather_words(2))
+
+        def load_docs(a, tag):
+            raw = sb([P, PACK, S], F32, "docs%d" % a, tag)
+            nc.sync.dma_start(raw[:], docs[512 * a : 512 * (a + 1), :].rearrange("(p j) w -> p j w", j=PACK))
+            return raw
+
+        docs_raw = [load_docs(0, "slot2")]
+
+        turned = bank(7, [P, P], "turned")
+        nc.tensor.transpose(turned[:], rows[:], ident[:])
+        vecs = sb([P, 3 * CT], F32, "vecs")
+        nc.vector.tensor_copy(vecs[:], turned[:, 0 : 3 * CT])
+        warm = sb([P, 1], F32, "warm")
+        nc.scalar.activation(warm[:], vecs[:, 0:1], SIGMOID)
+
+        def v_scale(a, lo, hi):
+            return v_plane[:, a * S + lo : a * S + hi]
+
+        sig = [sb([P, PACK, S], F32, "sig%d" % k) for k in range(RP)]
+        for c in range(CT):
+            acc = bank(c, [P, S], "a%d" % c)
+            for a in range(KP):
+                nc.tensor.matmul_mx(
+                    acc[:],
+                    lhsT=w4[a][:, c * 64 : (c + 1) * 64].bitcast(FP4X4),
+                    lhsT_scale=w4s[a][:].bitcast(U8)[:, c * P : (c + 1) * P],
+                    rhs=vs[a][:].bitcast(FP8X4),
+                    rhs_scale=v_scale(a, 0, S),
+                    start=(a == 0),
+                    stop=(a == KP - 1),
+                )
+            nc.scalar.activation(sig[c // PACK][:, c % PACK, :], acc[:], SIGMOID, bias=vecs[:, c : c + 1])
+
+        w8 = []
+        w8s = []
+        for a in range(KP):
+            ws = sb([P, H // 4], I32, "w8s_%d" % a)
+            permute(ws[:], ws_raw[:, a, :], 2)
+            w = sb([P, H], I32, "w8_%d" % a)
+            permute(w[:], w8_lo[:, a, :] if a < 2 else w8_hi[:, 0, :], 8)
+            w8.append(w)
+            w8s.append(ws)
+        docs_raw.append(load_docs(1, "slot0"))
+        docs_raw.append(load_docs(2, "slot1"))
+
+        def quantize(woven, name):
+            codes = sb([P, S], I32, name + "_codes")
+            plane = sb([P, S], U8, name + "_plane")
+            nc.vector.quantize_mx(codes[:].bitcast(FP8X4), plane[:], woven[:].rearrange("p n t -> p (n t)"))
+            return codes, plane
+
+        h_woven = []
+        for k in range(RP):
+            woven = sb([P, S, PACK], BF16, "h_woven%d" % k)
+            g = vecs[:, CT + PACK * k : CT + PACK * (k + 1)]
+            nc.vector.tensor_tensor(
+                woven[:].rearrange("p (n i) t -> p n t i", i=4),
+                sig[k][:].rearrange("p t (n i) -> p n t i", i=4),
+                g.unsqueeze(1).unsqueeze(3).to_broadcast([P, S // 4, PACK, 4]),
+                MULT,
+            )
+            h_woven.append(woven)
+        hq = [quantize(h_woven[k], "h%d" % k) for k in range(RP)]
+
+        bq = []
+        for k in range(RP):
+            woven = sb([P, S, PACK], BF16, "b_woven%d" % k)
+            bias = vecs[:, 2 * CT + PACK * k : 2 * CT + PACK * (k + 1)]
+            for n in range(MT):
+                acc = bank(MT * k + n, [P, PACK, P], "b%d_%d" % (k, n))
+                for t in range(PACK):
+                    c = PACK * k + t
+                    for a in range(KP):
+                        nc.tensor.matmul_mx(
+                            acc[:, t, :],
+                            lhsT=w8[a][:, c * P : (c + 1) * P].bitcast(FP8X4),
+                            lhsT_scale=w8s[a][:].bitcast(U8)[:, c * P : (c + 1) * P],
+                            rhs=vs[a][:, n * P : (n + 1) * P].bitcast(FP8X4),
+                            rhs_scale=v_scale(a, n * P, (n + 1) * P),
+                            start=(a == 0),
+                            stop=(a == KP - 1),
+                        )
+                nc.vector.tensor_tensor(
+                    woven[:, n * P : (n + 1) * P, :],
+                    acc[:].rearrange("p t n -> p n t"),
+                    bias.unsqueeze(1).to_broadcast([P, P, PACK]),
+                    ADD,
+                )
+            bq.append(quantize(woven, "b%d" % k))
+
+        dq = []
+        for a in range(KP):
+            woven = sb([P, S, PACK], BF16, "d_woven%d" % a)
+            nc.scalar.copy(
+                woven[:].rearrange("p (n i) t -> p n t i", i=4),
+                docs_raw[a][:].rearrange("p t (n i) -> p n t i", i=4),
+            )
+            dq.append(quantize(woven, "d%d" % a))
+
+        for m in range(MT):
+            cols = slice(m * P, (m + 1) * P)
+            d_acc = bank(m, [P, S], "d%d" % m)
+            for a in range(KP):
+                nc.tensor.matmul_mx(
+                    d_acc[:],
+                    lhsT=dq[a][0][:, cols].bitcast(FP8X4),
+                    lhsT_scale=dq[a][1][:, cols],
+                    rhs=vs[a][:].bitcast(FP8X4),
+                    rhs_scale=v_scale(a, 0, S),
+                    start=(a == 0),
+                    stop=(a == KP - 1),
+                )
+            d_sb = sb([P, S], F32, "d_sb%d" % m)
+            nc.scalar.copy(d_sb[:], d_acc[:])
+            e_acc = bank(MT + m, [P, S], "e%d" % m)
+            for k in range(RP):
+                nc.tensor.matmul_mx(
+                    e_acc[:],
+                    lhsT=hq[k][0][:, cols].bitcast(FP8X4),
+                    lhsT_scale=hq[k][1][:, cols],
+                    rhs=bq[k][0][:].bitcast(FP8X4),
+                    rhs_scale=bq[k][1][:],
+                    start=(k == 0),
+                    stop=(k == RP - 1),
+                )
+            res = sb([P, S], F32, "res%d" % m)
+            nc.vector.tensor_tensor(res[:], e_acc[:], d_sb[:], MULT)
+            nc.sync.dma_start(out[cols, :], res[:])

@@ -1,7 +1,6 @@
 from contextlib import ExitStack
 
 import concourse.mybir as mybir
-from concourse.masks import make_identity
 
 K, H, T, S = 1536, 1024, 2048, 512
 FLOPS = 2 * K * H * S * 2 + 2 * K * S * S + 2 * H * S * S
@@ -45,25 +44,32 @@ def tile_list_repository_matrix_kernel(
         offsets = keep.tile([P, S // 16], U16, name="offsets")
         nc.sync.dma_start(offsets[:], offs)
 
+        rows = sb([P, 32], F32, "rows")
+        nc.gpsimd.memset(rows[:], 0.0)
+        for n, vec in enumerate((b1, gain, b2)):
+            nc.sync.dma_start(
+                rows[n:P:4, :].rearrange("u (g i) -> u g i", i=RUN),
+                vec.rearrange("(g u i) -> u g i", u=32, i=RUN),
+            )
+
         win_tags = ["slot1", "slot2", "win2"]
         wins = []
         ws_raw = sb([P, KP, H // 4], I32, "ws_raw")
 
-        def load_w_scales(queue, scales):
+        def load_w_scales(queues, scales):
             for d in range(4):
-                queue.dma_start(
+                queues[d].dma_start(
                     ws_raw[32 * d : 32 * d + 4, :, :],
                     scales.bitcast(I32)[:, 4 * d : 4 * d + 4, :].rearrange("a r n -> r a n"),
                 )
 
         for a in range(KP):
             win = sb([P, T], U8, "win%d" % a, win_tags[a])
-            nc.vector.memset(win[:].bitcast(I32), 0)
+            (nc.gpsimd if a == 0 else nc.vector).memset(win[:].bitcast(I32), 0)
             nc.scalar.dma_start(win[0:P:8, :].bitcast(I32), tab_scales[a].bitcast(I32))
             wins.append(win)
-            if a == 0:
-                nc.vector.memset(ws_raw[:], 0)
-                load_w_scales(nc.gpsimd, w4_scales)
+        nc.vector.memset(ws_raw[:], 0)
+        load_w_scales([nc.gpsimd, nc.scalar, nc.scalar, nc.scalar], w4_scales)
 
         w4_raw = sb([P, KP, H // 2], I32, "w4_raw")
         nc.sync.dma_start(w4_raw[:], w4_words.bitcast(I32).rearrange("a p n -> p a n"))
@@ -78,15 +84,6 @@ def tile_list_repository_matrix_kernel(
         v_plane = sb([P, KP * S], U8, "v_plane")
         nc.vector.memset(v_plane[:].bitcast(I32), 0)
 
-        ident = sb([P, P], F32, "ident")
-        make_identity(nc, ident[:])
-        rows = sb([P, P], F32, "rows")
-        nc.vector.memset(rows[:], 0.0)
-        for n, vec in enumerate((b1, gain, b2)):
-            nc.gpsimd.dma_start(
-                rows[CT * n : CT * (n + 1), :].rearrange("c (g i) -> c g i", i=RUN),
-                vec.rearrange("(g c i) -> c g i", c=CT, i=RUN),
-            )
 
         picked = sb([P, KP * S], U8, "picked")
         tabs = [tab0]
@@ -99,8 +96,8 @@ def tile_list_repository_matrix_kernel(
 
         def permute(dst, src, words):
             nc.vector.tensor_copy(
-                dst.rearrange("p (c g w) -> p c g w", c=CT, w=words),
-                src.rearrange("p (g c w) -> p c g w", c=CT, w=words),
+                dst.rearrange("p (c q g w) -> p c q g w", c=CT, q=4, w=words),
+                src.rearrange("p (g q c w) -> p c q g w", c=CT, q=4, w=words),
             )
 
         def gather_words(a):
@@ -109,6 +106,10 @@ def tile_list_repository_matrix_kernel(
             return v
 
         vs = [gather_words(0)]
+        vecs = sb([P, CT, 4], F32, "vecs")
+        nc.vector.transpose(vecs[:].rearrange("p c v -> p (c v)"), rows[:])
+        warm = sb([P, 1], F32, "warm")
+        nc.scalar.activation(warm[:], vecs[:, 0, 0:1], SIGMOID)
         w4 = []
         w4s = []
         for a in range(KP):
@@ -122,7 +123,7 @@ def tile_list_repository_matrix_kernel(
         w8_all = w8_words.rearrange("a p n i -> p a (n i)").bitcast(I32)
         w8_lo = sb([P, 2, H], I32, "w8_lo", "slot0")
         nc.sync.dma_start(w8_lo[:], w8_all[:, 0:2, :])
-        load_w_scales(nc.scalar, w8_scales)
+        load_w_scales([nc.scalar] * 4, w8_scales)
         vs.append(gather_words(1))
         w8_hi = sb([P, 1, H], I32, "w8_hi", "slot1")
         nc.sync.dma_start(w8_hi[:], w8_all[:, 2:3, :])
@@ -135,30 +136,26 @@ def tile_list_repository_matrix_kernel(
 
         docs_raw = [load_docs(0, "slot2")]
 
-        turned = bank(7, [P, P], "turned")
-        nc.tensor.transpose(turned[:], rows[:], ident[:])
-        vecs = sb([P, 3 * CT], F32, "vecs")
-        nc.vector.tensor_copy(vecs[:], turned[:, 0 : 3 * CT])
-        warm = sb([P, 1], F32, "warm")
-        nc.scalar.activation(warm[:], vecs[:, 0:1], SIGMOID)
-
         def v_scale(a, lo, hi):
             return v_plane[:, a * S + lo : a * S + hi]
+
+        def a_pass(acc, c, a):
+            nc.tensor.matmul_mx(
+                acc[:],
+                lhsT=w4[a][:, c * 64 : (c + 1) * 64].bitcast(FP4X4),
+                lhsT_scale=w4s[a][:].bitcast(U8)[:, c * P : (c + 1) * P],
+                rhs=vs[a][:].bitcast(FP8X4),
+                rhs_scale=v_scale(a, 0, S),
+                start=(a == 0),
+                stop=(a == KP - 1),
+            )
 
         sig = [sb([P, PACK, S], F32, "sig%d" % k) for k in range(RP)]
         for c in range(CT):
             acc = bank(c, [P, S], "a%d" % c)
             for a in range(KP):
-                nc.tensor.matmul_mx(
-                    acc[:],
-                    lhsT=w4[a][:, c * 64 : (c + 1) * 64].bitcast(FP4X4),
-                    lhsT_scale=w4s[a][:].bitcast(U8)[:, c * P : (c + 1) * P],
-                    rhs=vs[a][:].bitcast(FP8X4),
-                    rhs_scale=v_scale(a, 0, S),
-                    start=(a == 0),
-                    stop=(a == KP - 1),
-                )
-            nc.scalar.activation(sig[c // PACK][:, c % PACK, :], acc[:], SIGMOID, bias=vecs[:, c : c + 1])
+                a_pass(acc, c, a)
+            nc.scalar.activation(sig[c // PACK][:, c % PACK, :], acc[:], SIGMOID, bias=vecs[:, c, 0:1])
 
         w8 = []
         w8s = []
@@ -181,7 +178,7 @@ def tile_list_repository_matrix_kernel(
         h_woven = []
         for k in range(RP):
             woven = sb([P, S, PACK], BF16, "h_woven%d" % k)
-            g = vecs[:, CT + PACK * k : CT + PACK * (k + 1)]
+            g = vecs[:, PACK * k : PACK * (k + 1), 1]
             nc.vector.tensor_tensor(
                 woven[:].rearrange("p (n i) t -> p n t i", i=4),
                 sig[k][:].rearrange("p t (n i) -> p n t i", i=4),
@@ -194,7 +191,7 @@ def tile_list_repository_matrix_kernel(
         bq = []
         for k in range(RP):
             woven = sb([P, S, PACK], BF16, "b_woven%d" % k)
-            bias = vecs[:, 2 * CT + PACK * k : 2 * CT + PACK * (k + 1)]
+            bias = vecs[:, PACK * k : PACK * (k + 1), 2]
             for n in range(MT):
                 acc = bank(MT * k + n, [P, PACK, P], "b%d_%d" % (k, n))
                 for t in range(PACK):

@@ -15,6 +15,7 @@ FP8X4 = mybir.dt.float8_e4m3fn_x4
 FP4X4 = mybir.dt.float4_e2m1fn_x4
 MULT = mybir.AluOpType.mult
 ADD = mybir.AluOpType.add
+IDENTITY = mybir.ActivationFunctionType.Identity
 SIGMOID = mybir.ActivationFunctionType.Sigmoid
 
 P = 128
@@ -25,6 +26,13 @@ CT = H // P
 GROUPS = 16
 RUN = 8
 MT = S // P
+AT_DOCS1 = 0
+AT_W8S = AT_DOCS1 + 4 * PACK * S
+AT_TAB2 = AT_W8S - 512
+AT_W4S = AT_TAB2 + 4 * T
+AT_W8_HI = AT_W4S + KP * H
+AT_W8_LO = AT_W8_HI + 4 * H
+AT_TAB0 = AT_W4S - 512
 
 
 def tile_list_repository_matrix_kernel(
@@ -33,16 +41,30 @@ def tile_list_repository_matrix_kernel(
     nc = tc.nc
     with ExitStack() as ctx:
         keep = ctx.enter_context(tc.tile_pool(name="keep", bufs=1))
+        shared = ctx.enter_context(tc.tile_pool(name="shared", bufs=1))
         psum = ctx.enter_context(tc.psum_pool(name="psum", bufs=1))
 
         def sb(shape, dtype, name, tag=None):
             return keep.tile(shape, dtype, name=name, tag=tag or name, align_bytes=64)
+
+        def placed(shape, dtype, name, offset):
+            return shared.tile(shape, dtype, name=name, tag=name, align_bytes=64, offset=offset)
 
         def bank(n, shape, name):
             return psum.tile(shape, F32, name=name, tag="bank%d" % n)
 
         offsets = keep.tile([P, S // 16], U16, name="offsets")
         nc.sync.dma_start(offsets[:], offs)
+
+        def load_window(dst, a, copies):
+            src = tab_scales[a].bitcast(I32).unsqueeze(1).to_broadcast([16, copies, T // 4])
+            nc.sync.dma_start(dst.bitcast(I32), src)
+
+        win_a = sb([P, T], U8, "win_a")
+        win_b = sb([P, T], U8, "win_b", "slot1")
+        load_window(win_a[0:P:2, :], 0, 4)
+        load_window(win_a[1:P:2, :], 1, 4)
+        load_window(win_b[:], 2, 8)
 
         rows = sb([P, 32], F32, "rows")
         nc.gpsimd.memset(rows[:], 0.0)
@@ -52,47 +74,40 @@ def tile_list_repository_matrix_kernel(
                 vec.rearrange("(g u i) -> u g i", u=32, i=RUN),
             )
 
-        win_tags = ["slot1", "slot2", "win2"]
-        wins = []
-        ws_raw = sb([P, KP, H // 4], I32, "ws_raw")
+        w4s_raw = sb([P, KP, H // 4], I32, "w4s_raw")
+        w8s_raw = sb([P, KP, H // 4], I32, "w8s_raw")
+        nc.vector.memset(w4s_raw[:], 0)
+        nc.vector.memset(w8s_raw[:], 0)
+        v_plane0 = sb([P, S], U8, "v_plane0")
+        v_plane12 = sb([P, 2 * S], U8, "v_plane12")
+        nc.vector.memset(v_plane0[:].bitcast(I32), 0)
+        nc.vector.memset(v_plane12[:].bitcast(I32), 0)
 
-        def load_w_scales(queues, scales):
+        def load_w_scales(queues, raw, scales):
             for d in range(4):
                 queues[d].dma_start(
-                    ws_raw[32 * d : 32 * d + 4, :, :],
+                    raw[32 * d : 32 * d + 4, :, :],
                     scales.bitcast(I32)[:, 4 * d : 4 * d + 4, :].rearrange("a r n -> r a n"),
                 )
 
-        for a in range(KP):
-            win = sb([P, T], U8, "win%d" % a, win_tags[a])
-            (nc.gpsimd if a == 0 else nc.vector).memset(win[:].bitcast(I32), 0)
-            nc.scalar.dma_start(win[0:P:8, :].bitcast(I32), tab_scales[a].bitcast(I32))
-            wins.append(win)
-        nc.vector.memset(ws_raw[:], 0)
-        load_w_scales([nc.gpsimd, nc.scalar, nc.scalar, nc.scalar], w4_scales)
-
-        w4_raw = sb([P, KP, H // 2], I32, "w4_raw")
-        nc.sync.dma_start(w4_raw[:], w4_words.bitcast(I32).rearrange("a p n -> p a n"))
-
-        def load_tab(a, tag):
-            tab = sb([P, T], I32, "tab%d" % a, tag)
+        def load_tab(a, tab):
             nc.sync.dma_start(tab[:], tab_words[a].rearrange("p t i -> p (t i)").bitcast(I32))
             return tab
 
-        tab0 = load_tab(0, "slot0")
+        tabs = [load_tab(0, placed([P, T], I32, "tab0", AT_TAB0))]
+        w4_raw = sb([P, KP, H // 2], I32, "w4_raw")
+        nc.sync.dma_start(w4_raw[:], w4_words.bitcast(I32).rearrange("a p n -> p a n"))
+        load_w_scales([nc.gpsimd, nc.gpsimd, nc.sync, nc.sync], w4s_raw, w4_scales)
+        load_w_scales([nc.gpsimd] * 4, w8s_raw, w8_scales)
 
-        v_plane = sb([P, KP * S], U8, "v_plane")
-        nc.vector.memset(v_plane[:].bitcast(I32), 0)
-
-
-        picked = sb([P, KP * S], U8, "picked")
-        tabs = [tab0]
-        for a in range(KP):
-            nc.vector.tensor_copy(picked[:, a * S : (a + 1) * S], wins[a][:].indirect(offsets[:]))
-            if a + 1 < KP:
-                tabs.append(load_tab(a + 1, win_tags[a]))
+        picked = sb([P, 2 * S], U8, "picked")
+        nc.vector.tensor_copy(picked[:, 0:S], win_a[:].indirect(offsets[:]))
+        nc.vector.tensor_copy(picked[:, S : 2 * S], win_b[:].indirect(offsets[:]))
         for r in range(4):
-            nc.scalar.dma_start(v_plane[r:P:32, :].bitcast(I32), picked[8 * r : P : 32, :].bitcast(I32))
+            nc.sync.dma_start(v_plane0[r:P:32, :].bitcast(I32), picked[8 * r : P : 32, 0:S].bitcast(I32))
+        tabs.append(load_tab(1, sb([P, T], I32, "tab1", "slot1")))
+        for r in range(4):
+            nc.sync.dma_start(v_plane12[r:P:32, :].bitcast(I32), picked[8 * r + 1 : P : 32, :].bitcast(I32))
 
         def permute(dst, src, words):
             nc.vector.tensor_copy(
@@ -106,38 +121,38 @@ def tile_list_repository_matrix_kernel(
             return v
 
         vs = [gather_words(0)]
-        vecs = sb([P, CT, 4], F32, "vecs")
-        nc.vector.transpose(vecs[:].rearrange("p c v -> p (c v)"), rows[:])
-        warm = sb([P, 1], F32, "warm")
-        nc.scalar.activation(warm[:], vecs[:, 0, 0:1], SIGMOID)
+        tabs.append(load_tab(2, placed([P, T], I32, "tab2", AT_TAB2)))
         w4 = []
         w4s = []
         for a in range(KP):
-            ws = sb([P, H // 4], I32, "w4s_%d" % a)
-            permute(ws[:], ws_raw[:, a, :], 2)
+            ws = placed([P, H // 4], I32, "w4s_%d" % a, AT_W4S + a * H)
+            permute(ws[:], w4s_raw[:, a, :], 2)
             w = sb([P, H // 2], I32, "w4_%d" % a)
             permute(w[:], w4_raw[:, a, :], 4)
             w4.append(w)
             w4s.append(ws)
 
         w8_all = w8_words.rearrange("a p n i -> p a (n i)").bitcast(I32)
-        w8_lo = sb([P, 2, H], I32, "w8_lo", "slot0")
+        w8_lo = placed([P, 2, H], I32, "w8_lo", AT_W8_LO)
         nc.sync.dma_start(w8_lo[:], w8_all[:, 0:2, :])
-        load_w_scales([nc.scalar] * 4, w8_scales)
-        vs.append(gather_words(1))
-        w8_hi = sb([P, 1, H], I32, "w8_hi", "slot1")
+        w8_hi = placed([P, 1, H], I32, "w8_hi", AT_W8_HI)
         nc.sync.dma_start(w8_hi[:], w8_all[:, 2:3, :])
+        vs.append(gather_words(1))
         vs.append(gather_words(2))
 
-        def load_docs(a, tag):
-            raw = sb([P, PACK, S], F32, "docs%d" % a, tag)
+        vecs = sb([P, CT, 4], F32, "vecs")
+        nc.vector.transpose(vecs[:].rearrange("p c v -> p (c v)"), rows[:])
+
+        def load_docs(a, raw):
             nc.sync.dma_start(raw[:], docs[512 * a : 512 * (a + 1), :].rearrange("(p j) w -> p j w", j=PACK))
             return raw
 
-        docs_raw = [load_docs(0, "slot2")]
+        docs_raw = [load_docs(0, sb([P, PACK, S], F32, "docs0", "slot1"))]
 
         def v_scale(a, lo, hi):
-            return v_plane[:, a * S + lo : a * S + hi]
+            if a == 0:
+                return v_plane0[:, lo:hi]
+            return v_plane12[:, (a - 1) * S + lo : (a - 1) * S + hi]
 
         def a_pass(acc, c, a):
             nc.tensor.matmul_mx(
@@ -160,71 +175,110 @@ def tile_list_repository_matrix_kernel(
         w8 = []
         w8s = []
         for a in range(KP):
-            ws = sb([P, H // 4], I32, "w8s_%d" % a)
-            permute(ws[:], ws_raw[:, a, :], 2)
+            ws = placed([P, H // 4], I32, "w8s_%d" % a, AT_W8S + a * H)
+            permute(ws[:], w8s_raw[:, a, :], 2)
             w = sb([P, H], I32, "w8_%d" % a)
             permute(w[:], w8_lo[:, a, :] if a < 2 else w8_hi[:, 0, :], 8)
             w8.append(w)
             w8s.append(ws)
-        docs_raw.append(load_docs(1, "slot0"))
-        docs_raw.append(load_docs(2, "slot1"))
+        docs_raw.append(load_docs(1, placed([P, PACK, S], F32, "docs1", AT_DOCS1)))
+        docs_raw.append(load_docs(2, placed([P, PACK, S], F32, "docs2", AT_W8_LO)))
 
-        def quantize(woven, name):
-            codes = sb([P, S], I32, name + "_codes")
-            plane = sb([P, S], U8, name + "_plane")
-            nc.vector.quantize_mx(codes[:].bitcast(FP8X4), plane[:], woven[:].rearrange("p n t -> p (n t)"))
-            return codes, plane
+        def quantized(name):
+            return sb([P, S], I32, name + "_codes"), sb([P, S], U8, name + "_plane")
 
-        h_woven = []
-        for k in range(RP):
-            woven = sb([P, S, PACK], BF16, "h_woven%d" % k)
-            g = vecs[:, PACK * k : PACK * (k + 1), 1]
-            nc.vector.tensor_tensor(
-                woven[:].rearrange("p (n i) t -> p n t i", i=4),
-                sig[k][:].rearrange("p t (n i) -> p n t i", i=4),
-                g.unsqueeze(1).unsqueeze(3).to_broadcast([P, S // 4, PACK, 4]),
-                MULT,
+        def quantize(dst, woven, cols):
+            nc.vector.quantize_mx(
+                dst[0][:, cols].bitcast(FP8X4), dst[1][:, cols], woven[:, cols, :].rearrange("p n t -> p (n t)")
             )
-            h_woven.append(woven)
-        hq = [quantize(h_woven[k], "h%d" % k) for k in range(RP)]
 
-        bq = []
-        for k in range(RP):
+        everything = slice(0, S)
+
+        def b_pass(acc, c, a, cols):
+            nc.tensor.matmul_mx(
+                acc,
+                lhsT=w8[a][:, c * P : (c + 1) * P].bitcast(FP8X4),
+                lhsT_scale=w8s[a][:].bitcast(U8)[:, c * P : (c + 1) * P],
+                rhs=vs[a][:, cols].bitcast(FP8X4),
+                rhs_scale=v_scale(a, cols.start, cols.stop),
+                start=(a == 0),
+                stop=(a == KP - 1),
+            )
+
+        def second_product_by_tiles(k):
+            flat = sb([P, PACK, S], BF16, "b_flat%d" % k)
+            for t in range(PACK):
+                c = PACK * k + t
+                acc = bank(t, [P, S], "b%d" % c)
+                for a in range(KP):
+                    b_pass(acc[:], c, a, everything)
+                nc.scalar.activation(flat[:, t, :], acc[:], IDENTITY, bias=vecs[:, c, 2:3])
+            woven = sb([P, S, PACK], BF16, "b_woven%d" % k)
+            nc.vector.tensor_copy(
+                woven[:].rearrange("p (n i) t -> p n t i", i=4), flat[:].rearrange("p t (n i) -> p n t i", i=4)
+            )
+            dst = quantized("b%d" % k)
+            quantize(dst, woven, everything)
+            return dst
+
+        def second_product(k):
             woven = sb([P, S, PACK], BF16, "b_woven%d" % k)
             bias = vecs[:, PACK * k : PACK * (k + 1), 2]
             for n in range(MT):
-                acc = bank(MT * k + n, [P, PACK, P], "b%d_%d" % (k, n))
+                acc = bank(PACK + n, [P, PACK, P], "b%d_%d" % (k, n))
                 for t in range(PACK):
-                    c = PACK * k + t
                     for a in range(KP):
-                        nc.tensor.matmul_mx(
-                            acc[:, t, :],
-                            lhsT=w8[a][:, c * P : (c + 1) * P].bitcast(FP8X4),
-                            lhsT_scale=w8s[a][:].bitcast(U8)[:, c * P : (c + 1) * P],
-                            rhs=vs[a][:, n * P : (n + 1) * P].bitcast(FP8X4),
-                            rhs_scale=v_scale(a, n * P, (n + 1) * P),
-                            start=(a == 0),
-                            stop=(a == KP - 1),
-                        )
+                        b_pass(acc[:, t, :], PACK * k + t, a, slice(n * P, (n + 1) * P))
                 nc.vector.tensor_tensor(
                     woven[:, n * P : (n + 1) * P, :],
                     acc[:].rearrange("p t n -> p n t"),
                     bias.unsqueeze(1).to_broadcast([P, P, PACK]),
                     ADD,
                 )
-            bq.append(quantize(woven, "b%d" % k))
+            dst = quantized("b%d" % k)
+            quantize(dst, woven, everything)
+            return dst
 
-        dq = []
-        for a in range(KP):
-            woven = sb([P, S, PACK], BF16, "d_woven%d" % a)
-            nc.scalar.copy(
-                woven[:].rearrange("p (n i) t -> p n t i", i=4),
-                docs_raw[a][:].rearrange("p t (n i) -> p n t i", i=4),
+        def weave_h(woven, k, cols):
+            width = cols.stop - cols.start
+            g = vecs[:, PACK * k : PACK * (k + 1), 1]
+            nc.vector.tensor_tensor(
+                woven[:, cols, :].rearrange("p (n i) t -> p n t i", i=4),
+                sig[k][:, :, cols].rearrange("p t (n i) -> p n t i", i=4),
+                g.unsqueeze(1).unsqueeze(3).to_broadcast([P, width // 4, PACK, 4]),
+                MULT,
             )
-            dq.append(quantize(woven, "d%d" % a))
 
-        for m in range(MT):
+        bq = [second_product_by_tiles(0)]
+
+        def weave_docs(woven, a, cols):
+            nc.scalar.copy(
+                woven[:, cols, :].rearrange("p (n i) t -> p n t i", i=4),
+                docs_raw[a][:, :, cols].rearrange("p t (n i) -> p n t i", i=4),
+            )
+
+        d_woven = [sb([P, S, PACK], BF16, "d_woven%d" % a, "w4_2" if a == 0 else None) for a in range(KP)]
+        dq = [quantized("d%d" % a) for a in range(KP)]
+        for a in range(KP - 1):
+            weave_docs(d_woven[a], a, everything)
+            quantize(dq[a], d_woven[a], everything)
+
+        bq.append(second_product(1))
+
+        h_woven = [placed([P, S, PACK], BF16, "h_woven0", AT_W8_HI), sb([P, S, PACK], BF16, "h_woven1")]
+        hq = [quantized("h%d" % k) for k in range(RP)]
+        weave_h(h_woven[0], 0, everything)
+        quantize(hq[0], h_woven[0], everything)
+
+        def prepare(m):
             cols = slice(m * P, (m + 1) * P)
+            weave_docs(d_woven[KP - 1], KP - 1, cols)
+            weave_h(h_woven[1], 1, cols)
+            quantize(dq[KP - 1], d_woven[KP - 1], cols)
+
+        def multiply(m):
+            cols = slice(m * P, (m + 1) * P)
+            quantize(hq[1], h_woven[1], cols)
             d_acc = bank(m, [P, S], "d%d" % m)
             for a in range(KP):
                 nc.tensor.matmul_mx(
@@ -236,9 +290,7 @@ def tile_list_repository_matrix_kernel(
                     start=(a == 0),
                     stop=(a == KP - 1),
                 )
-            d_sb = sb([P, S], F32, "d_sb%d" % m)
-            nc.scalar.copy(d_sb[:], d_acc[:])
-            e_acc = bank(MT + m, [P, S], "e%d" % m)
+            e_acc = bank(PACK + m, [P, S], "e%d" % m)
             for k in range(RP):
                 nc.tensor.matmul_mx(
                     e_acc[:],
@@ -249,6 +301,20 @@ def tile_list_repository_matrix_kernel(
                     start=(k == 0),
                     stop=(k == RP - 1),
                 )
+            return d_acc, e_acc
+
+        def finish(m, d_acc, e_acc):
+            d_sb = sb([P, S], F32, "d_sb%d" % m)
+            nc.scalar.copy(d_sb[:], d_acc[:])
             res = sb([P, S], F32, "res%d" % m)
             nc.vector.tensor_tensor(res[:], e_acc[:], d_sb[:], MULT)
-            nc.sync.dma_start(out[cols, :], res[:])
+            nc.sync.dma_start(out[m * P : (m + 1) * P, :], res[:])
+
+        sums = []
+        for step in range(MT + 2):
+            if step < MT:
+                prepare(step)
+            if 1 <= step <= MT:
+                sums.append(multiply(step - 1))
+            if step >= 2:
+                finish(step - 2, *sums[step - 2])

@@ -26,9 +26,7 @@ CT = H // P
 GROUPS = 16
 RUN = 8
 MT = S // P
-AT_DOCS1 = 0
-AT_W8S = AT_DOCS1 + 4 * PACK * S
-AT_TAB2 = AT_W8S - 512
+AT_TAB2 = 0
 AT_W4S = AT_TAB2 + 4 * T
 AT_W8_HI = AT_W4S + KP * H
 AT_W8_LO = AT_W8_HI + 4 * H
@@ -75,7 +73,7 @@ def tile_list_repository_matrix_kernel(
             )
 
         w4s_raw = sb([P, KP, H // 4], I32, "w4s_raw")
-        w8s_raw = sb([P, KP, H // 4], I32, "w8s_raw")
+        w8s_raw = sb([P, H // 4], I32, "w8s_raw")
         nc.vector.memset(w4s_raw[:], 0)
         nc.vector.memset(w8s_raw[:], 0)
         v_plane0 = sb([P, S], U8, "v_plane0")
@@ -98,7 +96,10 @@ def tile_list_repository_matrix_kernel(
         w4_raw = sb([P, KP, H // 2], I32, "w4_raw")
         nc.sync.dma_start(w4_raw[:], w4_words.bitcast(I32).rearrange("a p n -> p a n"))
         load_w_scales([nc.gpsimd, nc.gpsimd, nc.sync, nc.sync], w4s_raw, w4_scales)
-        load_w_scales([nc.gpsimd] * 4, w8s_raw, w8_scales)
+        for d in range(4):
+            nc.gpsimd.dma_start(
+                w8s_raw[32 * d : 32 * d + 4 * KP, :], w8_scales.bitcast(I32)[:, 4 * d : 4 * d + 4, :]
+            )
 
         picked = sb([P, 2 * S], U8, "picked")
         nc.vector.tensor_copy(picked[:, 0:S], win_a[:].indirect(offsets[:]))
@@ -173,16 +174,14 @@ def tile_list_repository_matrix_kernel(
             nc.scalar.activation(sig[c // PACK][:, c % PACK, :], acc[:], SIGMOID, bias=vecs[:, c, 0:1])
 
         w8 = []
-        w8s = []
         for a in range(KP):
-            ws = placed([P, H // 4], I32, "w8s_%d" % a, AT_W8S + a * H)
-            permute(ws[:], w8s_raw[:, a, :], 2)
             w = sb([P, H], I32, "w8_%d" % a)
             permute(w[:], w8_lo[:, a, :] if a < 2 else w8_hi[:, 0, :], 8)
             w8.append(w)
-            w8s.append(ws)
-        docs_raw.append(load_docs(1, placed([P, PACK, S], F32, "docs1", AT_DOCS1)))
-        docs_raw.append(load_docs(2, placed([P, PACK, S], F32, "docs2", AT_W8_LO)))
+        w8s = placed([P, H // 4], I32, "w8s", AT_W8_HI)
+        permute(w8s[:], w8s_raw[:], 2)
+        docs_raw.append(load_docs(1, placed([P, PACK, S], F32, "docs1", AT_TAB2)))
+        docs_raw.append(load_docs(2, placed([P, PACK, S], F32, "docs2", AT_W8_LO + H)))
 
         def quantized(name):
             return sb([P, S], I32, name + "_codes"), sb([P, S], U8, name + "_plane")
@@ -198,7 +197,7 @@ def tile_list_repository_matrix_kernel(
             nc.tensor.matmul_mx(
                 acc,
                 lhsT=w8[a][:, c * P : (c + 1) * P].bitcast(FP8X4),
-                lhsT_scale=w8s[a][:].bitcast(U8)[:, c * P : (c + 1) * P],
+                lhsT_scale=w8s[:].bitcast(U8)[4 * a : P, c * P : (c + 1) * P],
                 rhs=vs[a][:, cols].bitcast(FP8X4),
                 rhs_scale=v_scale(a, cols.start, cols.stop),
                 start=(a == 0),
@@ -265,7 +264,7 @@ def tile_list_repository_matrix_kernel(
 
         bq.append(second_product(1))
 
-        h_woven = [placed([P, S, PACK], BF16, "h_woven0", AT_W8_HI), sb([P, S, PACK], BF16, "h_woven1")]
+        h_woven = [placed([P, S, PACK], BF16, "h_woven0", AT_W8_HI + H), sb([P, S, PACK], BF16, "h_woven1")]
         hq = [quantized("h%d" % k) for k in range(RP)]
         weave_h(h_woven[0], 0, everything)
         quantize(hq[0], h_woven[0], everything)

@@ -26,11 +26,13 @@ CT = H // P
 GROUPS = 16
 RUN = 8
 MT = S // P
-AT_TAB2 = 0
-AT_W4S = AT_TAB2 + 4 * T
-AT_W8_HI = AT_W4S + KP * H
-AT_W8_LO = AT_W8_HI + 4 * H
-AT_TAB0 = AT_W4S - 512
+WARM = 3
+AT_TAB1 = 0
+AT_TAB2 = AT_TAB1 + 4 * T
+AT_PICKED = AT_TAB2 - S // 2
+AT_W8_LO = AT_TAB2 + 4 * T
+AT_W8_HI = AT_W8_LO + 8 * H
+AT_W4S_RAW = AT_W8_HI + 6 * H
 
 
 def tile_list_repository_matrix_kernel(
@@ -54,32 +56,32 @@ def tile_list_repository_matrix_kernel(
         offsets = keep.tile([P, S // 16], U16, name="offsets")
         nc.sync.dma_start(offsets[:], offs)
 
-        def load_window(dst, a, copies):
-            src = tab_scales[a].bitcast(I32).unsqueeze(1).to_broadcast([16, copies, T // 4])
-            nc.sync.dma_start(dst.bitcast(I32), src)
-
-        win_a = sb([P, T], U8, "win_a")
-        win_b = sb([P, T], U8, "win_b", "slot1")
-        load_window(win_a[0:P:2, :], 0, 4)
-        load_window(win_a[1:P:2, :], 1, 4)
-        load_window(win_b[:], 2, 8)
+        window = sb([P, T], U8, "window")
+        tab_rows = tab_scales.bitcast(I32)
+        first_two = tab_rows[0:2].rearrange("a q n -> q a n")
+        nc.sync.dma_start(window[0:P:4, :].bitcast(I32), first_two)
+        nc.sync.dma_start(window[1:P:2, :].bitcast(I32), tab_rows[2].unsqueeze(1).to_broadcast([16, 4, T // 4]))
+        nc.sync.dma_start(window[2:P:4, :].bitcast(I32), first_two)
 
         rows = sb([P, 32], F32, "rows")
         nc.gpsimd.memset(rows[:], 0.0)
-        for n, vec in enumerate((b1, gain, b2)):
-            nc.sync.dma_start(
-                rows[n:P:4, :].rearrange("u (g i) -> u g i", i=RUN),
+
+        def load_vector(queue, dst, n, vec):
+            queue.dma_start(
+                dst[n:P:4, :].rearrange("u (g i) -> u g i", i=RUN),
                 vec.rearrange("(g u i) -> u g i", u=32, i=RUN),
             )
 
-        w4s_raw = sb([P, KP, H // 4], I32, "w4s_raw")
+        load_vector(nc.sync, rows, 0, b1)
+        load_vector(nc.sync, rows, 1, gain)
+
+        w4s_raw = placed([P, KP, H // 4], I32, "w4s_raw", AT_W4S_RAW)
         w8s_raw = sb([P, H // 4], I32, "w8s_raw")
         nc.vector.memset(w4s_raw[:], 0)
         nc.vector.memset(w8s_raw[:], 0)
-        v_plane0 = sb([P, S], U8, "v_plane0")
-        v_plane12 = sb([P, 2 * S], U8, "v_plane12")
-        nc.vector.memset(v_plane0[:].bitcast(I32), 0)
-        nc.vector.memset(v_plane12[:].bitcast(I32), 0)
+        v_planes = [sb([P, S], U8, "v_plane%d" % a) for a in range(KP)]
+        for plane in v_planes[1:]:
+            nc.vector.memset(plane[:].bitcast(I32), 0)
 
         def load_w_scales(queues, raw, scales):
             for d in range(4):
@@ -92,23 +94,27 @@ def tile_list_repository_matrix_kernel(
             nc.sync.dma_start(tab[:], tab_words[a].rearrange("p t i -> p (t i)").bitcast(I32))
             return tab
 
-        tabs = [load_tab(0, placed([P, T], I32, "tab0", AT_TAB0))]
-        w4_raw = sb([P, KP, H // 2], I32, "w4_raw")
+        tabs = [load_tab(0, placed([P, T], I32, "tab0", AT_W8_LO))]
+        w4_raw = placed([P, KP, H // 2], I32, "w4_raw", AT_W8_HI)
         nc.sync.dma_start(w4_raw[:], w4_words.bitcast(I32).rearrange("a p n -> p a n"))
         load_w_scales([nc.gpsimd, nc.gpsimd, nc.sync, nc.sync], w4s_raw, w4_scales)
-        for d in range(4):
-            nc.gpsimd.dma_start(
-                w8s_raw[32 * d : 32 * d + 4 * KP, :], w8_scales.bitcast(I32)[:, 4 * d : 4 * d + 4, :]
-            )
+        for d, queue in enumerate((nc.gpsimd, nc.gpsimd, nc.gpsimd, nc.sync)):
+            queue.dma_start(w8s_raw[32 * d : 32 * d + 4 * KP, :], w8_scales.bitcast(I32)[:, 4 * d : 4 * d + 4, :])
 
-        picked = sb([P, 2 * S], U8, "picked")
-        nc.vector.tensor_copy(picked[:, 0:S], win_a[:].indirect(offsets[:]))
-        nc.vector.tensor_copy(picked[:, S : 2 * S], win_b[:].indirect(offsets[:]))
-        for r in range(4):
-            nc.sync.dma_start(v_plane0[r:P:32, :].bitcast(I32), picked[8 * r : P : 32, 0:S].bitcast(I32))
-        tabs.append(load_tab(1, sb([P, T], I32, "tab1", "slot1")))
-        for r in range(4):
-            nc.sync.dma_start(v_plane12[r:P:32, :].bitcast(I32), picked[8 * r + 1 : P : 32, :].bitcast(I32))
+        picked = placed([P, S], U8, "picked", AT_PICKED)
+        nc.vector.tensor_copy(picked[:], window[:].indirect(offsets[:]))
+        staged = sb([P, S], U8, "staged")
+        nc.vector.tensor_copy(staged[:].bitcast(I32), picked[:].bitcast(I32))
+        nc.vector.tensor_copy(v_planes[0][:].bitcast(I32), picked[:].bitcast(I32))
+        for r in range(1, 4):
+            nc.sync.dma_start(v_planes[0][r:P:32, :].bitcast(I32), staged[8 * r : P : 32, :].bitcast(I32))
+        for a in range(1, KP):
+            tabs.append(load_tab(a, placed([P, T], I32, "tab%d" % a, (AT_TAB1, AT_TAB2)[a - 1])))
+            for r in range(4):
+                nc.sync.dma_start(
+                    v_planes[a][r:P:32, :].bitcast(I32),
+                    staged[8 * r + 3 + a : P : 32, :].bitcast(I32),
+                )
 
         def permute(dst, src, words):
             nc.vector.tensor_copy(
@@ -122,11 +128,10 @@ def tile_list_repository_matrix_kernel(
             return v
 
         vs = [gather_words(0)]
-        tabs.append(load_tab(2, placed([P, T], I32, "tab2", AT_TAB2)))
         w4 = []
         w4s = []
         for a in range(KP):
-            ws = placed([P, H // 4], I32, "w4s_%d" % a, AT_W4S + a * H)
+            ws = sb([P, H // 4], I32, "w4s_%d" % a)
             permute(ws[:], w4s_raw[:, a, :], 2)
             w = sb([P, H // 2], I32, "w4_%d" % a)
             permute(w[:], w4_raw[:, a, :], 4)
@@ -138,6 +143,9 @@ def tile_list_repository_matrix_kernel(
         nc.sync.dma_start(w8_lo[:], w8_all[:, 0:2, :])
         w8_hi = placed([P, 1, H], I32, "w8_hi", AT_W8_HI)
         nc.sync.dma_start(w8_hi[:], w8_all[:, 2:3, :])
+        late_rows = placed([P, 32], F32, "late_rows", AT_W4S_RAW)
+        nc.vector.memset(late_rows[:], 0.0)
+        load_vector(nc.sync, late_rows, 2, b2)
         vs.append(gather_words(1))
         vs.append(gather_words(2))
 
@@ -148,12 +156,10 @@ def tile_list_repository_matrix_kernel(
             nc.sync.dma_start(raw[:], docs[512 * a : 512 * (a + 1), :].rearrange("(p j) w -> p j w", j=PACK))
             return raw
 
-        docs_raw = [load_docs(0, sb([P, PACK, S], F32, "docs0", "slot1"))]
+        docs_raw = [load_docs(0, placed([P, PACK, S], F32, "docs0", AT_TAB1))]
 
         def v_scale(a, lo, hi):
-            if a == 0:
-                return v_plane0[:, lo:hi]
-            return v_plane12[:, (a - 1) * S + lo : (a - 1) * S + hi]
+            return v_planes[a][:, lo:hi]
 
         def a_pass(acc, c, a):
             nc.tensor.matmul_mx(
@@ -167,11 +173,23 @@ def tile_list_repository_matrix_kernel(
             )
 
         sig = [sb([P, PACK, S], F32, "sig%d" % k) for k in range(RP)]
-        for c in range(CT):
-            acc = bank(c, [P, S], "a%d" % c)
-            for a in range(KP):
-                a_pass(acc, c, a)
-            nc.scalar.activation(sig[c // PACK][:, c % PACK, :], acc[:], SIGMOID, bias=vecs[:, c, 0:1])
+        for n in range(WARM):
+            warm = bank(CT - WARM + n, [P, S], "warm%d" % n)
+            nc.tensor.matmul_mx(
+                warm[:],
+                lhsT=vs[0][:, 0:P].bitcast(FP8X4),
+                lhsT_scale=staged[:, 0:P],
+                rhs=vs[0][:].bitcast(FP8X4),
+                rhs_scale=staged[:],
+                start=True,
+                stop=True,
+            )
+        accs = [bank(c, [P, S], "a%d" % c) for c in range(CT)]
+        for a in range(KP):
+            for c in range(CT):
+                a_pass(accs[c], c, a)
+                if a == KP - 1:
+                    nc.scalar.activation(sig[c // PACK][:, c % PACK, :], accs[c][:], SIGMOID, bias=vecs[:, c, 0:1])
 
         w8 = []
         for a in range(KP):
@@ -180,8 +198,10 @@ def tile_list_repository_matrix_kernel(
             w8.append(w)
         w8s = placed([P, H // 4], I32, "w8s", AT_W8_HI)
         permute(w8s[:], w8s_raw[:], 2)
+        late_vecs = placed([P, CT, 4], F32, "late_vecs", AT_W8_HI + H)
+        nc.vector.transpose(late_vecs[:].rearrange("p c v -> p (c v)"), late_rows[:])
         docs_raw.append(load_docs(1, placed([P, PACK, S], F32, "docs1", AT_TAB2)))
-        docs_raw.append(load_docs(2, placed([P, PACK, S], F32, "docs2", AT_W8_LO + H)))
+        docs_raw.append(load_docs(2, placed([P, PACK, S], F32, "docs2", AT_W8_LO)))
 
         def quantized(name):
             return sb([P, S], I32, name + "_codes"), sb([P, S], U8, name + "_plane")
@@ -211,7 +231,7 @@ def tile_list_repository_matrix_kernel(
                 acc = bank(t, [P, S], "b%d" % c)
                 for a in range(KP):
                     b_pass(acc[:], c, a, everything)
-                nc.scalar.activation(flat[:, t, :], acc[:], IDENTITY, bias=vecs[:, c, 2:3])
+                nc.scalar.activation(flat[:, t, :], acc[:], IDENTITY, bias=late_vecs[:, c, 2:3])
             woven = sb([P, S, PACK], BF16, "b_woven%d" % k)
             nc.vector.tensor_copy(
                 woven[:].rearrange("p (n i) t -> p n t i", i=4), flat[:].rearrange("p t (n i) -> p n t i", i=4)
@@ -222,7 +242,7 @@ def tile_list_repository_matrix_kernel(
 
         def second_product(k):
             woven = sb([P, S, PACK], BF16, "b_woven%d" % k)
-            bias = vecs[:, PACK * k : PACK * (k + 1), 2]
+            bias = late_vecs[:, PACK * k : PACK * (k + 1), 2]
             for n in range(MT):
                 acc = bank(PACK + n, [P, PACK, P], "b%d_%d" % (k, n))
                 for t in range(PACK):
@@ -256,28 +276,16 @@ def tile_list_repository_matrix_kernel(
                 docs_raw[a][:, :, cols].rearrange("p t (n i) -> p n t i", i=4),
             )
 
-        d_woven = [sb([P, S, PACK], BF16, "d_woven%d" % a, "w4_2" if a == 0 else None) for a in range(KP)]
+        d_woven = [sb([P, S, PACK], BF16, "d_woven%d" % a) for a in range(KP)]
         dq = [quantized("d%d" % a) for a in range(KP)]
-        for a in range(KP - 1):
-            weave_docs(d_woven[a], a, everything)
-            quantize(dq[a], d_woven[a], everything)
-
-        bq.append(second_product(1))
-
-        h_woven = [placed([P, S, PACK], BF16, "h_woven0", AT_W8_HI + H), sb([P, S, PACK], BF16, "h_woven1")]
-        hq = [quantized("h%d" % k) for k in range(RP)]
-        weave_h(h_woven[0], 0, everything)
-        quantize(hq[0], h_woven[0], everything)
-
-        def prepare(m):
+        halves = [slice(0, S // 2), slice(S // 2, S)]
+        for a in range(KP):
+            for cols in halves if a == KP - 1 else [everything]:
+                weave_docs(d_woven[a], a, cols)
+                quantize(dq[a], d_woven[a], cols)
+        d_sb = []
+        for m in range(MT):
             cols = slice(m * P, (m + 1) * P)
-            weave_docs(d_woven[KP - 1], KP - 1, cols)
-            weave_h(h_woven[1], 1, cols)
-            quantize(dq[KP - 1], d_woven[KP - 1], cols)
-
-        def multiply(m):
-            cols = slice(m * P, (m + 1) * P)
-            quantize(hq[1], h_woven[1], cols)
             d_acc = bank(m, [P, S], "d%d" % m)
             for a in range(KP):
                 nc.tensor.matmul_mx(
@@ -289,6 +297,23 @@ def tile_list_repository_matrix_kernel(
                     start=(a == 0),
                     stop=(a == KP - 1),
                 )
+            d_tile = sb([P, S], F32, "d_sb%d" % m)
+            nc.scalar.copy(d_tile[:], d_acc[:])
+            d_sb.append(d_tile)
+
+        bq.append(second_product(1))
+
+        h_woven = [sb([P, S, PACK], BF16, "h_woven0"), sb([P, S, PACK], BF16, "h_woven1")]
+        hq = [quantized("h%d" % k) for k in range(RP)]
+        weave_h(h_woven[0], 0, everything)
+        quantize(hq[0], h_woven[0], everything)
+
+        def prepare(m):
+            weave_h(h_woven[1], 1, slice(m * P, (m + 1) * P))
+
+        def multiply(m):
+            cols = slice(m * P, (m + 1) * P)
+            quantize(hq[1], h_woven[1], cols)
             e_acc = bank(PACK + m, [P, S], "e%d" % m)
             for k in range(RP):
                 nc.tensor.matmul_mx(
@@ -300,13 +325,11 @@ def tile_list_repository_matrix_kernel(
                     start=(k == 0),
                     stop=(k == RP - 1),
                 )
-            return d_acc, e_acc
+            return e_acc
 
-        def finish(m, d_acc, e_acc):
-            d_sb = sb([P, S], F32, "d_sb%d" % m)
-            nc.scalar.copy(d_sb[:], d_acc[:])
+        def finish(m, e_acc):
             res = sb([P, S], F32, "res%d" % m)
-            nc.vector.tensor_tensor(res[:], e_acc[:], d_sb[:], MULT)
+            nc.vector.tensor_tensor(res[:], e_acc[:], d_sb[m][:], MULT)
             nc.sync.dma_start(out[m * P : (m + 1) * P, :], res[:])
 
         sums = []
@@ -316,4 +339,4 @@ def tile_list_repository_matrix_kernel(
             if 1 <= step <= MT:
                 sums.append(multiply(step - 1))
             if step >= 2:
-                finish(step - 2, *sums[step - 2])
+                finish(step - 2, sums[step - 2])

@@ -242,7 +242,9 @@ def tile_list_repository_matrix_kernel(
 
         def second_product(k):
             woven = sb([P, S, PACK], BF16, "b_woven%d" % k)
-            bias = late_vecs[:, PACK * k : PACK * (k + 1), 2]
+            bias_line = sb([P, PACK], F32, "bias_line")
+            nc.vector.tensor_copy(bias_line[:], late_vecs[:, PACK * k : PACK * (k + 1), 2])
+            bias = bias_line[:]
             for n in range(MT):
                 acc = bank(PACK + n, [P, PACK, P], "b%d_%d" % (k, n))
                 for t in range(PACK):
@@ -258,14 +260,16 @@ def tile_list_repository_matrix_kernel(
             quantize(dst, woven, everything)
             return dst
 
+        h_flat = [sb([P, PACK, S], BF16, "h_flat%d" % k) for k in range(RP)]
+
+        def scale_h(k):
+            for t in range(PACK):
+                nc.vector.tensor_scalar_mul(h_flat[k][:, t, :], sig[k][:, t, :], vecs[:, PACK * k + t, 1:2])
+
         def weave_h(woven, k, cols):
-            width = cols.stop - cols.start
-            g = vecs[:, PACK * k : PACK * (k + 1), 1]
-            nc.vector.tensor_tensor(
+            nc.vector.tensor_copy(
                 woven[:, cols, :].rearrange("p (n i) t -> p n t i", i=4),
-                sig[k][:, :, cols].rearrange("p t (n i) -> p n t i", i=4),
-                g.unsqueeze(1).unsqueeze(3).to_broadcast([P, width // 4, PACK, 4]),
-                MULT,
+                h_flat[k][:, :, cols].rearrange("p t (n i) -> p n t i", i=4),
             )
 
         bq = [second_product_by_tiles(0)]
@@ -305,7 +309,9 @@ def tile_list_repository_matrix_kernel(
 
         h_woven = [sb([P, S, PACK], BF16, "h_woven0"), sb([P, S, PACK], BF16, "h_woven1")]
         hq = [quantized("h%d" % k) for k in range(RP)]
+        scale_h(0)
         weave_h(h_woven[0], 0, everything)
+        scale_h(1)
         quantize(hq[0], h_woven[0], everything)
 
         def prepare(m):

@@ -26,13 +26,11 @@ CT = H // P
 GROUPS = 16
 RUN = 8
 MT = S // P
-WARM = 3
 AT_TAB1 = 0
 AT_TAB2 = AT_TAB1 + 4 * T
 AT_PICKED = AT_TAB2 - S // 2
 AT_W8_LO = AT_TAB2 + 4 * T
 AT_W8_HI = AT_W8_LO + 8 * H
-AT_W4S_RAW = AT_W8_HI + 6 * H
 
 
 def tile_list_repository_matrix_kernel(
@@ -56,26 +54,20 @@ def tile_list_repository_matrix_kernel(
         offsets = keep.tile([P, S // 16], U16, name="offsets")
         nc.sync.dma_start(offsets[:], offs)
 
-        window = sb([P, T], U8, "window")
-        tab_rows = tab_scales.bitcast(I32)
-        first_two = tab_rows[0:2].rearrange("a q n -> q a n")
-        nc.sync.dma_start(window[0:P:4, :].bitcast(I32), first_two)
-        nc.sync.dma_start(window[1:P:2, :].bitcast(I32), tab_rows[2].unsqueeze(1).to_broadcast([16, 4, T // 4]))
-        nc.sync.dma_start(window[2:P:4, :].bitcast(I32), first_two)
-
         rows = sb([P, 32], F32, "rows")
+        window = sb([P, T], U8, "window")
         nc.gpsimd.memset(rows[:], 0.0)
-
-        def load_vector(queue, dst, n, vec):
-            queue.dma_start(
-                dst[n:P:4, :].rearrange("u (g i) -> u g i", i=RUN),
+        nc.vector.memset(window[:].bitcast(I32), 0)
+        for n, vec in enumerate((b1, gain, b2)):
+            nc.sync.dma_start(
+                rows[n:P:4, :].rearrange("u (g i) -> u g i", i=RUN),
                 vec.rearrange("(g u i) -> u g i", u=32, i=RUN),
             )
+        tab_rows = tab_scales.bitcast(I32)
+        nc.sync.dma_start(window[0:P:4, :].bitcast(I32), tab_rows[0:2].rearrange("a q n -> q a n"))
+        nc.sync.dma_start(window[5:P:8, :].bitcast(I32), tab_rows[2])
 
-        load_vector(nc.sync, rows, 0, b1)
-        load_vector(nc.sync, rows, 1, gain)
-
-        w4s_raw = placed([P, KP, H // 4], I32, "w4s_raw", AT_W4S_RAW)
+        w4s_raw = sb([P, KP, H // 4], I32, "w4s_raw")
         w8s_raw = sb([P, H // 4], I32, "w8s_raw")
         nc.vector.memset(w4s_raw[:], 0)
         nc.vector.memset(w8s_raw[:], 0)
@@ -143,9 +135,6 @@ def tile_list_repository_matrix_kernel(
         nc.sync.dma_start(w8_lo[:], w8_all[:, 0:2, :])
         w8_hi = placed([P, 1, H], I32, "w8_hi", AT_W8_HI)
         nc.sync.dma_start(w8_hi[:], w8_all[:, 2:3, :])
-        late_rows = placed([P, 32], F32, "late_rows", AT_W4S_RAW)
-        nc.vector.memset(late_rows[:], 0.0)
-        load_vector(nc.sync, late_rows, 2, b2)
         vs.append(gather_words(1))
         vs.append(gather_words(2))
 
@@ -173,17 +162,6 @@ def tile_list_repository_matrix_kernel(
             )
 
         sig = [sb([P, PACK, S], F32, "sig%d" % k) for k in range(RP)]
-        for n in range(WARM):
-            warm = bank(CT - WARM + n, [P, S], "warm%d" % n)
-            nc.tensor.matmul_mx(
-                warm[:],
-                lhsT=vs[0][:, 0:P].bitcast(FP8X4),
-                lhsT_scale=staged[:, 0:P],
-                rhs=vs[0][:].bitcast(FP8X4),
-                rhs_scale=staged[:],
-                start=True,
-                stop=True,
-            )
         accs = [bank(c, [P, S], "a%d" % c) for c in range(CT)]
         for a in range(KP):
             for c in range(CT):
@@ -198,8 +176,6 @@ def tile_list_repository_matrix_kernel(
             w8.append(w)
         w8s = placed([P, H // 4], I32, "w8s", AT_W8_HI)
         permute(w8s[:], w8s_raw[:], 2)
-        late_vecs = placed([P, CT, 4], F32, "late_vecs", AT_W8_HI + H)
-        nc.vector.transpose(late_vecs[:].rearrange("p c v -> p (c v)"), late_rows[:])
         docs_raw.append(load_docs(1, placed([P, PACK, S], F32, "docs1", AT_TAB2)))
         docs_raw.append(load_docs(2, placed([P, PACK, S], F32, "docs2", AT_W8_LO)))
 
@@ -228,10 +204,10 @@ def tile_list_repository_matrix_kernel(
             flat = sb([P, PACK, S], BF16, "b_flat%d" % k)
             for t in range(PACK):
                 c = PACK * k + t
-                acc = bank(t, [P, S], "b%d" % c)
+                acc = bank(c, [P, S], "b%d" % c)
                 for a in range(KP):
                     b_pass(acc[:], c, a, everything)
-                nc.scalar.activation(flat[:, t, :], acc[:], IDENTITY, bias=late_vecs[:, c, 2:3])
+                nc.scalar.activation(flat[:, t, :], acc[:], IDENTITY, bias=vecs[:, c, 2:3])
             woven = sb([P, S, PACK], BF16, "b_woven%d" % k)
             nc.vector.tensor_copy(
                 woven[:].rearrange("p (n i) t -> p n t i", i=4), flat[:].rearrange("p t (n i) -> p n t i", i=4)
@@ -243,10 +219,10 @@ def tile_list_repository_matrix_kernel(
         def second_product(k):
             woven = sb([P, S, PACK], BF16, "b_woven%d" % k)
             bias_line = sb([P, PACK], F32, "bias_line")
-            nc.vector.tensor_copy(bias_line[:], late_vecs[:, PACK * k : PACK * (k + 1), 2])
+            nc.vector.tensor_copy(bias_line[:], vecs[:, PACK * k : PACK * (k + 1), 2])
             bias = bias_line[:]
             for n in range(MT):
-                acc = bank(PACK + n, [P, PACK, P], "b%d_%d" % (k, n))
+                acc = bank(n, [P, PACK, P], "b%d_%d" % (k, n))
                 for t in range(PACK):
                     for a in range(KP):
                         b_pass(acc[:, t, :], PACK * k + t, a, slice(n * P, (n + 1) * P))
@@ -272,7 +248,7 @@ def tile_list_repository_matrix_kernel(
                 h_flat[k][:, :, cols].rearrange("p t (n i) -> p n t i", i=4),
             )
 
-        bq = [second_product_by_tiles(0)]
+        bq = [second_product(0), second_product_by_tiles(1)]
 
         def weave_docs(woven, a, cols):
             nc.scalar.copy(
@@ -304,8 +280,6 @@ def tile_list_repository_matrix_kernel(
             d_tile = sb([P, S], F32, "d_sb%d" % m)
             nc.scalar.copy(d_tile[:], d_acc[:])
             d_sb.append(d_tile)
-
-        bq.append(second_product(1))
 
         h_woven = [sb([P, S, PACK], BF16, "h_woven0"), sb([P, S, PACK], BF16, "h_woven1")]
         hq = [quantized("h%d" % k) for k in range(RP)]

@@ -28,7 +28,6 @@ RUN = 8
 MT = S // P
 AT_TAB1 = 0
 AT_TAB2 = AT_TAB1 + 4 * T
-AT_PICKED = AT_TAB2 - S // 2
 AT_W8_LO = AT_TAB2 + 4 * T
 AT_W8_HI = AT_W8_LO + 8 * H
 
@@ -55,25 +54,27 @@ def tile_list_repository_matrix_kernel(
         nc.sync.dma_start(offsets[:], offs)
 
         rows = sb([P, 32], F32, "rows")
-        window = sb([P, T], U8, "window")
+        win_a = sb([P, T], U8, "win_a")
+        win_b = sb([P, T], U8, "win_b")
         nc.gpsimd.memset(rows[:], 0.0)
-        nc.vector.memset(window[:].bitcast(I32), 0)
+        nc.vector.memset(win_a[:].bitcast(I32), 0)
+        nc.vector.memset(win_b[:].bitcast(I32), 0)
         for n, vec in enumerate((b1, gain, b2)):
             nc.sync.dma_start(
                 rows[n:P:4, :].rearrange("u (g i) -> u g i", i=RUN),
                 vec.rearrange("(g u i) -> u g i", u=32, i=RUN),
             )
         tab_rows = tab_scales.bitcast(I32)
-        nc.sync.dma_start(window[0:P:4, :].bitcast(I32), tab_rows[0:2].rearrange("a q n -> q a n"))
-        nc.sync.dma_start(window[5:P:8, :].bitcast(I32), tab_rows[2])
+        nc.sync.dma_start(win_a[0:P:4, :].bitcast(I32), tab_rows[0:2].rearrange("a q n -> q a n"))
+        nc.sync.dma_start(win_b[4:P:8, :].bitcast(I32), tab_rows[2])
 
         w4s_raw = sb([P, KP, H // 4], I32, "w4s_raw")
         w8s_raw = sb([P, H // 4], I32, "w8s_raw")
         nc.vector.memset(w4s_raw[:], 0)
         nc.vector.memset(w8s_raw[:], 0)
-        v_planes = [sb([P, S], U8, "v_plane%d" % a) for a in range(KP)]
-        for plane in v_planes[1:]:
-            nc.vector.memset(plane[:].bitcast(I32), 0)
+        plane_first = sb([P, S], U8, "plane_first")
+        planes_later = sb([P, 2 * S], U8, "planes_later")
+        nc.vector.memset(planes_later[:].bitcast(I32), 0)
 
         def load_w_scales(queues, raw, scales):
             for d in range(4):
@@ -89,24 +90,24 @@ def tile_list_repository_matrix_kernel(
         tabs = [load_tab(0, placed([P, T], I32, "tab0", AT_W8_LO))]
         w4_raw = placed([P, KP, H // 2], I32, "w4_raw", AT_W8_HI)
         nc.sync.dma_start(w4_raw[:], w4_words.bitcast(I32).rearrange("a p n -> p a n"))
-        load_w_scales([nc.gpsimd, nc.gpsimd, nc.sync, nc.sync], w4s_raw, w4_scales)
-        for d, queue in enumerate((nc.gpsimd, nc.gpsimd, nc.gpsimd, nc.sync)):
-            queue.dma_start(w8s_raw[32 * d : 32 * d + 4 * KP, :], w8_scales.bitcast(I32)[:, 4 * d : 4 * d + 4, :])
+        load_w_scales([nc.gpsimd, nc.sync, nc.sync, nc.sync], w4s_raw, w4_scales)
+        for d in range(4):
+            nc.gpsimd.dma_start(w8s_raw[32 * d : 32 * d + 4 * KP, :], w8_scales.bitcast(I32)[:, 4 * d : 4 * d + 4, :])
 
-        picked = placed([P, S], U8, "picked", AT_PICKED)
-        nc.vector.tensor_copy(picked[:], window[:].indirect(offsets[:]))
-        staged = sb([P, S], U8, "staged")
-        nc.vector.tensor_copy(staged[:].bitcast(I32), picked[:].bitcast(I32))
-        nc.vector.tensor_copy(v_planes[0][:].bitcast(I32), picked[:].bitcast(I32))
+        staged = sb([P, 2 * S], U8, "staged")
+        pick_a = placed([P, S], U8, "pick_a", AT_TAB1)
+        nc.vector.tensor_copy(pick_a[:], win_a[:].indirect(offsets[:]))
+        nc.vector.tensor_copy(staged[:, 0:S].bitcast(I32), pick_a[:].bitcast(I32))
+        nc.vector.tensor_copy(plane_first[:].bitcast(I32), pick_a[:].bitcast(I32))
         for r in range(1, 4):
-            nc.sync.dma_start(v_planes[0][r:P:32, :].bitcast(I32), staged[8 * r : P : 32, :].bitcast(I32))
-        for a in range(1, KP):
-            tabs.append(load_tab(a, placed([P, T], I32, "tab%d" % a, (AT_TAB1, AT_TAB2)[a - 1])))
-            for r in range(4):
-                nc.sync.dma_start(
-                    v_planes[a][r:P:32, :].bitcast(I32),
-                    staged[8 * r + 3 + a : P : 32, :].bitcast(I32),
-                )
+            nc.sync.dma_start(plane_first[r:P:32, :].bitcast(I32), staged[8 * r : P : 32, 0:S].bitcast(I32))
+        tabs.append(load_tab(1, placed([P, T], I32, "tab1", AT_TAB1)))
+        pick_b = placed([P, S], U8, "pick_b", AT_TAB2)
+        nc.vector.tensor_copy(pick_b[:], win_b[:].indirect(offsets[:]))
+        nc.vector.tensor_copy(staged[:, S : 2 * S].bitcast(I32), pick_b[:].bitcast(I32))
+        for r in range(4):
+            nc.sync.dma_start(planes_later[r:P:32, :].bitcast(I32), staged[8 * r + 4 : P : 32, :].bitcast(I32))
+        tabs.append(load_tab(2, placed([P, T], I32, "tab2", AT_TAB2)))
 
         def permute(dst, src, words):
             nc.vector.tensor_copy(
@@ -148,7 +149,9 @@ def tile_list_repository_matrix_kernel(
         docs_raw = [load_docs(0, placed([P, PACK, S], F32, "docs0", AT_TAB1))]
 
         def v_scale(a, lo, hi):
-            return v_planes[a][:, lo:hi]
+            if a == 0:
+                return plane_first[:, lo:hi]
+            return planes_later[:, (a - 1) * S + lo : (a - 1) * S + hi]
 
         def a_pass(acc, c, a):
             nc.tensor.matmul_mx(

@@ -29,7 +29,12 @@ MT = S // P
 AT_TAB1 = 0
 AT_TAB2 = AT_TAB1 + 4 * T
 AT_W8_LO = AT_TAB2 + 4 * T
-AT_W8_HI = AT_W8_LO + 8 * H
+AT_W4_2 = AT_W8_LO + 8 * H
+AT_STAGED = AT_W4_2 + 2 * H
+AT_WIN_A = AT_STAGED + 4 * H
+AT_W8_HI = AT_WIN_A + T
+W4S = KP * H // 4
+SW = S // 4
 
 
 def tile_list_repository_matrix_kernel(
@@ -53,61 +58,66 @@ def tile_list_repository_matrix_kernel(
         offsets = keep.tile([P, S // 16], U16, name="offsets")
         nc.sync.dma_start(offsets[:], offs)
 
+        w4_all = w4_words.bitcast(I32)
+        w4_early = placed([P, 2, H // 2], I32, "w4_early", AT_W8_HI)
+        nc.sync.dma_start(w4_early[:], w4_all[0:2].rearrange("a p n -> p a n"))
+        staged = placed([P, W4S + SW], I32, "staged", AT_STAGED)
+        staged_later = sb([P, 2 * SW], I32, "staged_later")
+        nc.sync.dma_start(
+            staged[0:P:8, 0:W4S].rearrange("q (a n) -> q a n", a=KP),
+            w4_scales.bitcast(I32).rearrange("a q n -> q a n"),
+        )
+
         rows = sb([P, 32], F32, "rows")
-        win_a = sb([P, T], U8, "win_a")
+        win_a = placed([P, T], U8, "win_a", AT_WIN_A)
         win_b = sb([P, T], U8, "win_b")
-        nc.gpsimd.memset(rows[:], 0.0)
+        nc.gpsimd.memset(win_b[:].bitcast(I32), 0)
+        nc.vector.memset(rows[:], 0.0)
         nc.vector.memset(win_a[:].bitcast(I32), 0)
-        nc.vector.memset(win_b[:].bitcast(I32), 0)
-        for n, vec in enumerate((b1, gain, b2)):
+
+        def load_vector(n, vec):
             nc.sync.dma_start(
                 rows[n:P:4, :].rearrange("u (g i) -> u g i", i=RUN),
                 vec.rearrange("(g u i) -> u g i", u=32, i=RUN),
             )
+
+        load_vector(0, b1)
+        load_vector(1, gain)
         tab_rows = tab_scales.bitcast(I32)
         nc.sync.dma_start(win_a[0:P:4, :].bitcast(I32), tab_rows[0:2].rearrange("a q n -> q a n"))
         nc.sync.dma_start(win_b[4:P:8, :].bitcast(I32), tab_rows[2])
 
-        w4s_raw = sb([P, KP, H // 4], I32, "w4s_raw")
         w8s_raw = sb([P, H // 4], I32, "w8s_raw")
-        nc.vector.memset(w4s_raw[:], 0)
-        nc.vector.memset(w8s_raw[:], 0)
-        plane_first = sb([P, S], U8, "plane_first")
+        planes_first = sb([P, W4S + SW], I32, "planes_first")
         planes_later = sb([P, 2 * S], U8, "planes_later")
+        nc.vector.memset(planes_first[:], 0)
+        nc.vector.memset(w8s_raw[:], 0)
         nc.vector.memset(planes_later[:].bitcast(I32), 0)
-
-        def load_w_scales(queues, raw, scales):
-            for d in range(4):
-                queues[d].dma_start(
-                    raw[32 * d : 32 * d + 4, :, :],
-                    scales.bitcast(I32)[:, 4 * d : 4 * d + 4, :].rearrange("a r n -> r a n"),
-                )
 
         def load_tab(a, tab):
             nc.sync.dma_start(tab[:], tab_words[a].rearrange("p t i -> p (t i)").bitcast(I32))
             return tab
 
         tabs = [load_tab(0, placed([P, T], I32, "tab0", AT_W8_LO))]
-        w4_raw = placed([P, KP, H // 2], I32, "w4_raw", AT_W8_HI)
-        nc.sync.dma_start(w4_raw[:], w4_words.bitcast(I32).rearrange("a p n -> p a n"))
-        load_w_scales([nc.gpsimd, nc.sync, nc.sync, nc.sync], w4s_raw, w4_scales)
+        tabs.append(load_tab(1, placed([P, T], I32, "tab1", AT_TAB1)))
+        load_vector(2, b2)
         for d in range(4):
             nc.gpsimd.dma_start(w8s_raw[32 * d : 32 * d + 4 * KP, :], w8_scales.bitcast(I32)[:, 4 * d : 4 * d + 4, :])
 
-        staged = sb([P, 2 * S], U8, "staged")
-        pick_a = placed([P, S], U8, "pick_a", AT_TAB1)
+        pick_a = placed([P, S], U8, "pick_a", AT_TAB2)
         nc.vector.tensor_copy(pick_a[:], win_a[:].indirect(offsets[:]))
-        nc.vector.tensor_copy(staged[:, 0:S].bitcast(I32), pick_a[:].bitcast(I32))
-        nc.vector.tensor_copy(plane_first[:].bitcast(I32), pick_a[:].bitcast(I32))
-        for r in range(1, 4):
-            nc.sync.dma_start(plane_first[r:P:32, :].bitcast(I32), staged[8 * r : P : 32, 0:S].bitcast(I32))
-        tabs.append(load_tab(1, placed([P, T], I32, "tab1", AT_TAB1)))
-        pick_b = placed([P, S], U8, "pick_b", AT_TAB2)
-        nc.vector.tensor_copy(pick_b[:], win_b[:].indirect(offsets[:]))
-        nc.vector.tensor_copy(staged[:, S : 2 * S].bitcast(I32), pick_b[:].bitcast(I32))
+        nc.vector.tensor_copy(staged[:, W4S : W4S + SW], pick_a[:].bitcast(I32))
+        nc.vector.tensor_copy(staged_later[:, 0:SW], pick_a[:].bitcast(I32))
         for r in range(4):
-            nc.sync.dma_start(planes_later[r:P:32, :].bitcast(I32), staged[8 * r + 4 : P : 32, :].bitcast(I32))
+            nc.scalar.dma_start(planes_first[r:P:32, :], staged[8 * r : P : 32, :])
         tabs.append(load_tab(2, placed([P, T], I32, "tab2", AT_TAB2)))
+        pick_b = placed([P, S], U8, "pick_b", AT_W4_2)
+        nc.vector.tensor_copy(pick_b[:], win_b[:].indirect(offsets[:]))
+        nc.vector.tensor_copy(staged_later[:, SW : 2 * SW], pick_b[:].bitcast(I32))
+        for r in range(4):
+            nc.scalar.dma_start(planes_later[r:P:32, :].bitcast(I32), staged_later[8 * r + 4 : P : 32, :])
+        w4_last = placed([P, H // 2], I32, "w4_last", AT_W4_2)
+        nc.sync.dma_start(w4_last[:], w4_all[2])
 
         def permute(dst, src, words):
             nc.vector.tensor_copy(
@@ -116,20 +126,29 @@ def tile_list_repository_matrix_kernel(
             )
 
         def gather_words(a):
-            v = sb([P, S], I32, "v%d" % a)
+            v = placed([P, S], I32, "v1", AT_STAGED) if a == 1 else sb([P, S], I32, "v%d" % a)
             nc.vector.tensor_copy(v[:].bitcast(U32), tabs[a][:].bitcast(U32).indirect(offsets[:]))
             return v
 
-        vs = [gather_words(0)]
         w4 = []
         w4s = []
-        for a in range(KP):
-            ws = sb([P, H // 4], I32, "w4s_%d" % a)
-            permute(ws[:], w4s_raw[:, a, :], 2)
-            w = sb([P, H // 2], I32, "w4_%d" % a)
-            permute(w[:], w4_raw[:, a, :], 4)
+
+        def order_w4(a):
+            if a == KP - 1:
+                w = sb([P, H // 2], I32, "w4_2")
+            else:
+                w = placed([P, H // 2], I32, "w4_%d" % a, (AT_WIN_A, AT_STAGED + 4 * S)[a])
+            permute(w[:], w4_early[:, a, :] if a < 2 else w4_last[:], 4)
             w4.append(w)
+
+        def order_w4_scales(a):
+            ws = sb([P, H // 4], I32, "w4s_%d" % a)
+            permute(ws[:], planes_first[:, a * H // 4 : (a + 1) * H // 4], 2)
             w4s.append(ws)
+
+        order_w4(0)
+        vs = [gather_words(0)]
+        order_w4_scales(0)
 
         w8_all = w8_words.rearrange("a p n i -> p a (n i)").bitcast(I32)
         w8_lo = placed([P, 2, H], I32, "w8_lo", AT_W8_LO)
@@ -137,7 +156,11 @@ def tile_list_repository_matrix_kernel(
         w8_hi = placed([P, 1, H], I32, "w8_hi", AT_W8_HI)
         nc.sync.dma_start(w8_hi[:], w8_all[:, 2:3, :])
         vs.append(gather_words(1))
+        order_w4_scales(1)
+        order_w4_scales(2)
+        order_w4(1)
         vs.append(gather_words(2))
+        order_w4(2)
 
         vecs = sb([P, CT, 4], F32, "vecs")
         nc.vector.transpose(vecs[:].rearrange("p c v -> p (c v)"), rows[:])
@@ -150,7 +173,7 @@ def tile_list_repository_matrix_kernel(
 
         def v_scale(a, lo, hi):
             if a == 0:
-                return plane_first[:, lo:hi]
+                return planes_first[:, W4S : W4S + SW].bitcast(U8)[:, lo:hi]
             return planes_later[:, (a - 1) * S + lo : (a - 1) * S + hi]
 
         def a_pass(acc, c, a):
@@ -166,11 +189,12 @@ def tile_list_repository_matrix_kernel(
 
         sig = [sb([P, PACK, S], F32, "sig%d" % k) for k in range(RP)]
         accs = [bank(c, [P, S], "a%d" % c) for c in range(CT)]
-        for a in range(KP):
-            for c in range(CT):
+        for c in range(CT):
+            a_pass(accs[c], c, 0)
+        for c in range(CT):
+            for a in range(1, KP):
                 a_pass(accs[c], c, a)
-                if a == KP - 1:
-                    nc.scalar.activation(sig[c // PACK][:, c % PACK, :], accs[c][:], SIGMOID, bias=vecs[:, c, 0:1])
+            nc.scalar.activation(sig[c // PACK][:, c % PACK, :], accs[c][:], SIGMOID, bias=vecs[:, c, 0:1])
 
         w8 = []
         for a in range(KP):

@@ -29,10 +29,8 @@ MT = S // P
 AT_TAB1 = 0
 AT_TAB2 = AT_TAB1 + 4 * T
 AT_W8_LO = AT_TAB2 + 4 * T
-AT_W4_2 = AT_W8_LO + 8 * H
-AT_STAGED = AT_W4_2 + 2 * H
-AT_WIN_A = AT_STAGED + 4 * H
-AT_W8_HI = AT_WIN_A + T
+AT_STAGED = AT_W8_LO + 8 * H
+AT_W8_HI = AT_STAGED + 4 * H
 W4S = KP * H // 4
 SW = S // 4
 
@@ -59,8 +57,8 @@ def tile_list_repository_matrix_kernel(
         nc.sync.dma_start(offsets[:], offs)
 
         w4_all = w4_words.bitcast(I32)
-        w4_early = placed([P, 2, H // 2], I32, "w4_early", AT_W8_HI)
-        nc.sync.dma_start(w4_early[:], w4_all[0:2].rearrange("a p n -> p a n"))
+        w4_first = sb([P, H // 2], I32, "w4_first")
+        nc.sync.dma_start(w4_first[:], w4_all[0])
         staged = placed([P, W4S + SW], I32, "staged", AT_STAGED)
         staged_later = sb([P, 2 * SW], I32, "staged_later")
         nc.sync.dma_start(
@@ -69,7 +67,7 @@ def tile_list_repository_matrix_kernel(
         )
 
         rows = sb([P, 32], F32, "rows")
-        win_a = placed([P, T], U8, "win_a", AT_WIN_A)
+        win_a = sb([P, T], U8, "win_a")
         win_b = sb([P, T], U8, "win_b")
         nc.gpsimd.memset(win_b[:].bitcast(I32), 0)
         nc.vector.memset(rows[:], 0.0)
@@ -99,25 +97,25 @@ def tile_list_repository_matrix_kernel(
             return tab
 
         tabs = [load_tab(0, placed([P, T], I32, "tab0", AT_W8_LO))]
-        tabs.append(load_tab(1, placed([P, T], I32, "tab1", AT_TAB1)))
+        w4_later = placed([P, 2, H // 2], I32, "w4_later", AT_W8_HI)
+        nc.sync.dma_start(w4_later[:], w4_all[1:KP].rearrange("a p n -> p a n"))
         load_vector(2, b2)
         for d in range(4):
             nc.gpsimd.dma_start(w8s_raw[32 * d : 32 * d + 4 * KP, :], w8_scales.bitcast(I32)[:, 4 * d : 4 * d + 4, :])
 
-        pick_a = placed([P, S], U8, "pick_a", AT_TAB2)
+        pick_a = placed([P, S], U8, "pick_a", AT_TAB1)
         nc.vector.tensor_copy(pick_a[:], win_a[:].indirect(offsets[:]))
         nc.vector.tensor_copy(staged[:, W4S : W4S + SW], pick_a[:].bitcast(I32))
         nc.vector.tensor_copy(staged_later[:, 0:SW], pick_a[:].bitcast(I32))
         for r in range(4):
-            nc.scalar.dma_start(planes_first[r:P:32, :], staged[8 * r : P : 32, :])
-        tabs.append(load_tab(2, placed([P, T], I32, "tab2", AT_TAB2)))
-        pick_b = placed([P, S], U8, "pick_b", AT_W4_2)
+            nc.sync.dma_start(planes_first[r:P:32, :], staged[8 * r : P : 32, :])
+        tabs.append(load_tab(1, placed([P, T], I32, "tab1", AT_TAB1)))
+        pick_b = placed([P, S], U8, "pick_b", AT_TAB2)
         nc.vector.tensor_copy(pick_b[:], win_b[:].indirect(offsets[:]))
         nc.vector.tensor_copy(staged_later[:, SW : 2 * SW], pick_b[:].bitcast(I32))
         for r in range(4):
-            nc.scalar.dma_start(planes_later[r:P:32, :].bitcast(I32), staged_later[8 * r + 4 : P : 32, :])
-        w4_last = placed([P, H // 2], I32, "w4_last", AT_W4_2)
-        nc.sync.dma_start(w4_last[:], w4_all[2])
+            nc.sync.dma_start(planes_later[r:P:32, :].bitcast(I32), staged_later[8 * r + 4 : P : 32, :])
+        tabs.append(load_tab(2, placed([P, T], I32, "tab2", AT_TAB2)))
 
         def permute(dst, src, words):
             nc.vector.tensor_copy(
@@ -126,7 +124,7 @@ def tile_list_repository_matrix_kernel(
             )
 
         def gather_words(a):
-            v = placed([P, S], I32, "v1", AT_STAGED) if a == 1 else sb([P, S], I32, "v%d" % a)
+            v = sb([P, S], I32, "v%d" % a)
             nc.vector.tensor_copy(v[:].bitcast(U32), tabs[a][:].bitcast(U32).indirect(offsets[:]))
             return v
 
@@ -134,11 +132,11 @@ def tile_list_repository_matrix_kernel(
         w4s = []
 
         def order_w4(a):
-            if a == KP - 1:
-                w = sb([P, H // 2], I32, "w4_2")
+            if a == 0:
+                w = sb([P, H // 2], I32, "w4_0")
             else:
-                w = placed([P, H // 2], I32, "w4_%d" % a, (AT_WIN_A, AT_STAGED + 4 * S)[a])
-            permute(w[:], w4_early[:, a, :] if a < 2 else w4_last[:], 4)
+                w = placed([P, H // 2], I32, "w4_%d" % a, AT_STAGED + (a - 1) * 2 * H)
+            permute(w[:], w4_first[:] if a == 0 else w4_later[:, a - 1, :], 4)
             w4.append(w)
 
         def order_w4_scales(a):
@@ -149,6 +147,10 @@ def tile_list_repository_matrix_kernel(
         order_w4(0)
         vs = [gather_words(0)]
         order_w4_scales(0)
+        order_w4_scales(1)
+        order_w4_scales(2)
+        order_w4(1)
+        order_w4(2)
 
         w8_all = w8_words.rearrange("a p n i -> p a (n i)").bitcast(I32)
         w8_lo = placed([P, 2, H], I32, "w8_lo", AT_W8_LO)
@@ -156,11 +158,7 @@ def tile_list_repository_matrix_kernel(
         w8_hi = placed([P, 1, H], I32, "w8_hi", AT_W8_HI)
         nc.sync.dma_start(w8_hi[:], w8_all[:, 2:3, :])
         vs.append(gather_words(1))
-        order_w4_scales(1)
-        order_w4_scales(2)
-        order_w4(1)
         vs.append(gather_words(2))
-        order_w4(2)
 
         vecs = sb([P, CT, 4], F32, "vecs")
         nc.vector.transpose(vecs[:].rearrange("p c v -> p (c v)"), rows[:])
@@ -279,8 +277,8 @@ def tile_list_repository_matrix_kernel(
 
         def weave_docs(woven, a, cols):
             nc.scalar.copy(
-                woven[:, cols, :].rearrange("p (n i) t -> p n t i", i=4),
-                docs_raw[a][:, :, cols].rearrange("p t (n i) -> p n t i", i=4),
+                woven[:, cols, :].rearrange("p (n i) t -> p n t i", i=2),
+                docs_raw[a][:, :, cols].rearrange("p t (n i) -> p n t i", i=2),
             )
 
         d_woven = [sb([P, S, PACK], BF16, "d_woven%d" % a) for a in range(KP)]

@@ -26,9 +26,10 @@ CT = H // P
 GROUPS = 16
 RUN = 8
 MT = S // P
+EARLY = 6
 AT_TAB1 = 0
 AT_TAB2 = AT_TAB1 + 4 * T
-AT_W8_LO = AT_TAB2 + 4 * T
+AT_W8_LO = AT_TAB2 + 4 * T + H
 AT_STAGED = AT_W8_LO + 8 * H
 AT_W8_HI = AT_STAGED + 4 * H
 W4S = KP * H // 4
@@ -117,10 +118,10 @@ def tile_list_repository_matrix_kernel(
             nc.sync.dma_start(planes_later[r:P:32, :].bitcast(I32), staged_later[8 * r + 4 : P : 32, :])
         tabs.append(load_tab(2, placed([P, T], I32, "tab2", AT_TAB2)))
 
-        def permute(dst, src, words):
+        def permute(dst, src, words, tiles=slice(0, CT)):
             nc.vector.tensor_copy(
-                dst.rearrange("p (c q g w) -> p c q g w", c=CT, q=4, w=words),
-                src.rearrange("p (g q c w) -> p c q g w", c=CT, q=4, w=words),
+                dst.rearrange("p (c q g w) -> p c q g w", q=4, g=4, w=words),
+                src.rearrange("p (g q c w) -> p c q g w", c=CT, q=4, w=words)[:, tiles],
             )
 
         def gather_words(a):
@@ -147,7 +148,9 @@ def tile_list_repository_matrix_kernel(
         order_w4(0)
         vs = [gather_words(0)]
         order_w4_scales(0)
-        order_w4_scales(1)
+        w4s_1lo = sb([P, EARLY * 32], I32, "w4s_1lo")
+        permute(w4s_1lo[:], planes_first[:, H // 4 : H // 2], 2, slice(0, EARLY))
+        w4s.append(None)
         order_w4_scales(2)
         order_w4(1)
         order_w4(2)
@@ -159,6 +162,15 @@ def tile_list_repository_matrix_kernel(
         nc.sync.dma_start(w8_hi[:], w8_all[:, 2:3, :])
         vs.append(gather_words(1))
         vs.append(gather_words(2))
+        w4s_1hi = placed([P, (CT - EARLY) * 32], I32, "w4s_1hi", AT_TAB2)
+        permute(w4s_1hi[:], planes_first[:, H // 4 : H // 2], 2, slice(EARLY, CT))
+
+        def w4_plane(a, c):
+            if a == 1 and c < EARLY:
+                return w4s_1lo[:].bitcast(U8)[:, c * P : (c + 1) * P]
+            if a == 1:
+                return w4s_1hi[:].bitcast(U8)[:, (c - EARLY) * P : (c - EARLY + 1) * P]
+            return w4s[a][:].bitcast(U8)[:, c * P : (c + 1) * P]
 
         vecs = sb([P, CT, 4], F32, "vecs")
         nc.vector.transpose(vecs[:].rearrange("p c v -> p (c v)"), rows[:])
@@ -178,7 +190,7 @@ def tile_list_repository_matrix_kernel(
             nc.tensor.matmul_mx(
                 acc[:],
                 lhsT=w4[a][:, c * 64 : (c + 1) * 64].bitcast(FP4X4),
-                lhsT_scale=w4s[a][:].bitcast(U8)[:, c * P : (c + 1) * P],
+                lhsT_scale=w4_plane(a, c),
                 rhs=vs[a][:].bitcast(FP8X4),
                 rhs_scale=v_scale(a, 0, S),
                 start=(a == 0),
@@ -201,7 +213,7 @@ def tile_list_repository_matrix_kernel(
             w8.append(w)
         w8s = placed([P, H // 4], I32, "w8s", AT_W8_HI)
         permute(w8s[:], w8s_raw[:], 2)
-        docs_raw.append(load_docs(1, placed([P, PACK, S], F32, "docs1", AT_TAB2)))
+        docs_raw.append(load_docs(1, placed([P, PACK, S], F32, "docs1", AT_TAB2 + H)))
         docs_raw.append(load_docs(2, placed([P, PACK, S], F32, "docs2", AT_W8_LO)))
 
         def quantized(name):
@@ -313,12 +325,8 @@ def tile_list_repository_matrix_kernel(
         scale_h(1)
         quantize(hq[0], h_woven[0], everything)
 
-        def prepare(m):
-            weave_h(h_woven[1], 1, slice(m * P, (m + 1) * P))
-
         def multiply(m):
             cols = slice(m * P, (m + 1) * P)
-            quantize(hq[1], h_woven[1], cols)
             e_acc = bank(PACK + m, [P, S], "e%d" % m)
             for k in range(RP):
                 nc.tensor.matmul_mx(
@@ -337,11 +345,11 @@ def tile_list_repository_matrix_kernel(
             nc.vector.tensor_tensor(res[:], e_acc[:], d_sb[m][:], MULT)
             nc.sync.dma_start(out[m * P : (m + 1) * P, :], res[:])
 
-        sums = []
-        for step in range(MT + 2):
-            if step < MT:
-                prepare(step)
-            if 1 <= step <= MT:
-                sums.append(multiply(step - 1))
-            if step >= 2:
-                finish(step - 2, sums[step - 2])
+        weave_h(h_woven[1], 1, halves[0])
+        weave_h(h_woven[1], 1, halves[1])
+        quantize(hq[1], h_woven[1], halves[0])
+        sums = [multiply(0), multiply(1)]
+        quantize(hq[1], h_woven[1], halves[1])
+        sums += [multiply(2), multiply(3)]
+        for m in range(MT):
+            finish(m, sums[m])

@@ -16,6 +16,7 @@ FP4X4 = mybir.dt.float4_e2m1fn_x4
 MULT = mybir.AluOpType.mult
 ADD = mybir.AluOpType.add
 IDENTITY = mybir.ActivationFunctionType.Identity
+COPY = mybir.ActivationFunctionType.Copy
 SIGMOID = mybir.ActivationFunctionType.Sigmoid
 
 P = 128
@@ -26,12 +27,14 @@ CT = H // P
 GROUPS = 16
 RUN = 8
 MT = S // P
+SCALAR_GAINS = 2
 EARLY = 6
 AT_TAB1 = 0
 AT_TAB2 = AT_TAB1 + 4 * T
 AT_W8_LO = AT_TAB2 + 4 * T + H
-AT_STAGED = AT_W8_LO + 8 * H
+AT_STAGED = AT_W8_LO + 9 * H
 AT_W8_HI = AT_STAGED + 4 * H
+AT_HALF = AT_W8_HI + 4 * H
 W4S = KP * H // 4
 SW = S // 4
 
@@ -89,8 +92,8 @@ def tile_list_repository_matrix_kernel(
         w8s_raw = sb([P, H // 4], I32, "w8s_raw")
         planes_first = sb([P, W4S + SW], I32, "planes_first")
         planes_later = sb([P, 2 * S], U8, "planes_later")
-        nc.vector.memset(planes_first[:], 0)
         nc.vector.memset(w8s_raw[:], 0)
+        nc.vector.memset(planes_first[:], 0)
         nc.vector.memset(planes_later[:].bitcast(I32), 0)
 
         def load_tab(a, tab):
@@ -209,12 +212,16 @@ def tile_list_repository_matrix_kernel(
         w8 = []
         for a in range(KP):
             w = sb([P, H], I32, "w8_%d" % a)
-            permute(w[:], w8_lo[:, a, :] if a < 2 else w8_hi[:, 0, :], 8)
+            if a < 2:
+                permute(w[:], w8_lo[:, a, :], 8)
+            else:
+                w8s = placed([P, H // 4], I32, "w8s", AT_W8_LO)
+                permute(w8s[:], w8s_raw[:], 2)
+                permute(w[:, 0 : H // 2], w8_hi[:, 0, :], 8, slice(0, PACK))
+                permute(w[:, H // 2 : H], w8_hi[:, 0, :], 8, slice(PACK, CT))
             w8.append(w)
-        w8s = placed([P, H // 4], I32, "w8s", AT_W8_HI)
-        permute(w8s[:], w8s_raw[:], 2)
         docs_raw.append(load_docs(1, placed([P, PACK, S], F32, "docs1", AT_TAB2 + H)))
-        docs_raw.append(load_docs(2, placed([P, PACK, S], F32, "docs2", AT_W8_LO)))
+        docs_raw.append(load_docs(2, placed([P, PACK, S], F32, "docs2", AT_W8_LO + H)))
 
         def quantized(name):
             return sb([P, S], I32, name + "_codes"), sb([P, S], U8, name + "_plane")
@@ -226,130 +233,128 @@ def tile_list_repository_matrix_kernel(
 
         everything = slice(0, S)
 
-        def b_pass(acc, c, a, cols):
+        def b_pass(acc, c, a, cols, start, stop):
             nc.tensor.matmul_mx(
                 acc,
                 lhsT=w8[a][:, c * P : (c + 1) * P].bitcast(FP8X4),
                 lhsT_scale=w8s[:].bitcast(U8)[4 * a : P, c * P : (c + 1) * P],
                 rhs=vs[a][:, cols].bitcast(FP8X4),
                 rhs_scale=v_scale(a, cols.start, cols.stop),
-                start=(a == 0),
-                stop=(a == KP - 1),
+                start=start,
+                stop=stop,
             )
 
-        def second_product_by_tiles(k):
-            flat = sb([P, PACK, S], BF16, "b_flat%d" % k)
-            for t in range(PACK):
-                c = PACK * k + t
-                acc = bank(c, [P, S], "b%d" % c)
-                for a in range(KP):
-                    b_pass(acc[:], c, a, everything)
-                nc.scalar.activation(flat[:, t, :], acc[:], IDENTITY, bias=vecs[:, c, 2:3])
-            woven = sb([P, S, PACK], BF16, "b_woven%d" % k)
-            nc.vector.tensor_copy(
-                woven[:].rearrange("p (n i) t -> p n t i", i=4), flat[:].rearrange("p t (n i) -> p n t i", i=4)
-            )
-            dst = quantized("b%d" % k)
-            quantize(dst, woven, everything)
-            return dst
+        def weave(copy, woven, flat, run):
+            copy(woven.rearrange("p (n i) t -> p n t i", i=run), flat.rearrange("p t (n i) -> p n t i", i=run))
 
-        def second_product(k):
-            woven = sb([P, S, PACK], BF16, "b_woven%d" % k)
-            bias_line = sb([P, PACK], F32, "bias_line")
-            nc.vector.tensor_copy(bias_line[:], vecs[:, PACK * k : PACK * (k + 1), 2])
-            bias = bias_line[:]
-            for n in range(MT):
-                acc = bank(n, [P, PACK, P], "b%d_%d" % (k, n))
-                for t in range(PACK):
-                    for a in range(KP):
-                        b_pass(acc[:, t, :], PACK * k + t, a, slice(n * P, (n + 1) * P))
-                nc.vector.tensor_tensor(
-                    woven[:, n * P : (n + 1) * P, :],
-                    acc[:].rearrange("p t n -> p n t"),
-                    bias.unsqueeze(1).to_broadcast([P, P, PACK]),
-                    ADD,
-                )
-            dst = quantized("b%d" % k)
-            quantize(dst, woven, everything)
-            return dst
-
+        b_woven = [sb([P, S, PACK], BF16, "b_woven%d" % k) for k in range(RP)]
+        h_woven = [sb([P, S, PACK], BF16, "h_woven%d" % k) for k in range(RP)]
+        d_woven = [sb([P, S, PACK], BF16, "d_woven%d" % a) for a in range(KP - 1)]
         h_flat = [sb([P, PACK, S], BF16, "h_flat%d" % k) for k in range(RP)]
+        b_flat = sb([P, PACK, S], BF16, "b_flat")
+        bq = [quantized("b%d" % k) for k in range(RP)]
+        dq = [quantized("d%d" % a) for a in range(KP)]
+        hq = [quantized("h%d" % k) for k in range(RP)]
+        halves = [slice(0, S // 2), slice(S // 2, S)]
 
-        def scale_h(k):
-            for t in range(PACK):
+        def quantize_half(dst, woven, cols):
+            nc.vector.quantize_mx(dst[0][:, cols].bitcast(FP8X4), dst[1][:, cols], woven[:].rearrange("p n t -> p (n t)"))
+
+        def scale_h(k, tiles):
+            for t in tiles:
                 nc.vector.tensor_scalar_mul(h_flat[k][:, t, :], sig[k][:, t, :], vecs[:, PACK * k + t, 1:2])
 
-        def weave_h(woven, k, cols):
-            nc.vector.tensor_copy(
-                woven[:, cols, :].rearrange("p (n i) t -> p n t i", i=4),
-                h_flat[k][:, :, cols].rearrange("p t (n i) -> p n t i", i=4),
-            )
-
-        bq = [second_product(0), second_product_by_tiles(1)]
-
-        def weave_docs(woven, a, cols):
-            nc.scalar.copy(
-                woven[:, cols, :].rearrange("p (n i) t -> p n t i", i=2),
-                docs_raw[a][:, :, cols].rearrange("p t (n i) -> p n t i", i=2),
-            )
-
-        d_woven = [sb([P, S, PACK], BF16, "d_woven%d" % a) for a in range(KP)]
-        dq = [quantized("d%d" % a) for a in range(KP)]
-        halves = [slice(0, S // 2), slice(S // 2, S)]
+        bias_first = placed([P, PACK], F32, "bias_first", AT_HALF)
+        bias_later = sb([P, PACK], F32, "bias_later")
+        nc.vector.tensor_copy(bias_first[:], vecs[:, 0:PACK, 2])
+        nc.vector.tensor_copy(bias_later[:], vecs[:, 0:PACK, 2])
+        sums = [bank(n, [P, PACK, P], "b0_%d" % n) for n in range(MT)]
         for a in range(KP):
-            for cols in halves if a == KP - 1 else [everything]:
-                weave_docs(d_woven[a], a, cols)
-                quantize(dq[a], d_woven[a], cols)
-        d_sb = []
-        for m in range(MT):
-            cols = slice(m * P, (m + 1) * P)
-            d_acc = bank(m, [P, S], "d%d" % m)
+            for n in range(MT):
+                for t in range(PACK):
+                    first, last = (a, t) == (0, 0), (a, t) == (KP - 1, PACK - 1)
+                    b_pass(sums[n][:, t, :], t, a, slice(n * P, (n + 1) * P), first, last)
+        for n in range(MT):
+            nc.vector.tensor_tensor(
+                b_woven[0][:, n * P : (n + 1) * P, :],
+                sums[n][:].rearrange("p t n -> p n t"),
+                (bias_later if n else bias_first)[:].unsqueeze(1).to_broadcast([P, P, PACK]),
+                ADD,
+            )
+
+        first_woven = [placed([P, S // 2, PACK], BF16, "d_first0", AT_HALF), sb([P, S // 2, PACK], BF16, "d_first1")]
+        nc.gpsimd.tensor_scalar(
+            first_woven[0][:], docs_raw[0][:, :, halves[0]].rearrange("p t n -> p n t"), 1.0, 0.0, MULT, ADD
+        )
+        weave(nc.scalar.copy, first_woven[1][:], docs_raw[0][:, :, halves[1]], 2)
+        for t in range(PACK - SCALAR_GAINS, PACK):
+            nc.scalar.activation(h_flat[1][:, t, :], sig[1][:, t, :], COPY, scale=vecs[:, PACK + t, 1:2])
+        weave(nc.scalar.copy, d_woven[0][:], docs_raw[1][:], 2)
+        for t in range(PACK):
+            acc = bank(PACK + t, [P, S], "b%d" % t)
             for a in range(KP):
-                nc.tensor.matmul_mx(
-                    d_acc[:],
-                    lhsT=dq[a][0][:, cols].bitcast(FP8X4),
-                    lhsT_scale=dq[a][1][:, cols],
-                    rhs=vs[a][:].bitcast(FP8X4),
-                    rhs_scale=v_scale(a, 0, S),
-                    start=(a == 0),
-                    stop=(a == KP - 1),
-                )
-            d_tile = sb([P, S], F32, "d_sb%d" % m)
-            nc.scalar.copy(d_tile[:], d_acc[:])
-            d_sb.append(d_tile)
+                b_pass(acc[:], PACK + t, a, everything, a == 0, a == KP - 1)
+            nc.scalar.activation(b_flat[:, t, :], acc[:], IDENTITY, bias=vecs[:, PACK + t, 2:3])
+        for cols in halves:
+            weave(nc.scalar.copy, d_woven[1][:, cols, :], docs_raw[2][:, :, cols], 2)
 
-        h_woven = [sb([P, S, PACK], BF16, "h_woven0"), sb([P, S, PACK], BF16, "h_woven1")]
-        hq = [quantized("h%d" % k) for k in range(RP)]
-        scale_h(0)
-        weave_h(h_woven[0], 0, everything)
-        scale_h(1)
+        scale_h(0, range(PACK))
+        weave(nc.vector.tensor_copy, h_woven[0][:], h_flat[0][:], 4)
+        quantize(bq[0], b_woven[0], everything)
+        quantize_half(dq[0], first_woven[1], halves[1])
+        quantize_half(dq[0], first_woven[0], halves[0])
+        quantize(dq[1], d_woven[0], everything)
         quantize(hq[0], h_woven[0], everything)
+        weave(nc.vector.tensor_copy, b_woven[1][:], b_flat[:], 4)
+        quantize(dq[2], d_woven[1], halves[0])
+        quantize(bq[1], b_woven[1], everything)
+        quantize(dq[2], d_woven[1], halves[1])
+        scale_h(1, range(PACK - SCALAR_GAINS))
+        for cols in halves:
+            weave(nc.vector.tensor_copy, h_woven[1][:, cols, :], h_flat[1][:, :, cols], 4)
+        for cols in halves:
+            quantize(hq[1], h_woven[1], cols)
 
-        def multiply(m):
+        def d_pass(acc, m, a, start, stop):
             cols = slice(m * P, (m + 1) * P)
-            e_acc = bank(PACK + m, [P, S], "e%d" % m)
-            for k in range(RP):
-                nc.tensor.matmul_mx(
-                    e_acc[:],
-                    lhsT=hq[k][0][:, cols].bitcast(FP8X4),
-                    lhsT_scale=hq[k][1][:, cols],
-                    rhs=bq[k][0][:].bitcast(FP8X4),
-                    rhs_scale=bq[k][1][:],
-                    start=(k == 0),
-                    stop=(k == RP - 1),
-                )
-            return e_acc
+            nc.tensor.matmul_mx(
+                acc[:],
+                lhsT=dq[a][0][:, cols].bitcast(FP8X4),
+                lhsT_scale=dq[a][1][:, cols],
+                rhs=vs[a][:].bitcast(FP8X4),
+                rhs_scale=v_scale(a, 0, S),
+                start=start,
+                stop=stop,
+            )
 
-        def finish(m, e_acc):
-            res = sb([P, S], F32, "res%d" % m)
-            nc.vector.tensor_tensor(res[:], e_acc[:], d_sb[m][:], MULT)
-            nc.sync.dma_start(out[m * P : (m + 1) * P, :], res[:])
+        def e_pass(acc, m, k):
+            cols = slice(m * P, (m + 1) * P)
+            nc.tensor.matmul_mx(
+                acc[:],
+                lhsT=hq[k][0][:, cols].bitcast(FP8X4),
+                lhsT_scale=hq[k][1][:, cols],
+                rhs=bq[k][0][:].bitcast(FP8X4),
+                rhs_scale=bq[k][1][:],
+                start=(k == 0),
+                stop=(k == RP - 1),
+            )
 
-        weave_h(h_woven[1], 1, halves[0])
-        weave_h(h_woven[1], 1, halves[1])
-        quantize(hq[1], h_woven[1], halves[0])
-        sums = [multiply(0), multiply(1)]
-        quantize(hq[1], h_woven[1], halves[1])
-        sums += [multiply(2), multiply(3)]
+        d_accs = [bank(m, [P, S], "d%d" % m) for m in range(MT)]
+        e_accs = [bank(PACK + m, [P, S], "e%d" % m) for m in range(MT)]
+        for a in range(KP - 1):
+            for m in range(MT):
+                d_pass(d_accs[m], m, a, a == 0, False)
         for m in range(MT):
-            finish(m, sums[m])
+            e_pass(e_accs[m], m, 0)
+        for pair in range(MT // 2):
+            tiles = (2 * pair, 2 * pair + 1)
+            d_sb = {}
+            for m in tiles:
+                d_pass(d_accs[m], m, 2, False, True)
+                d_sb[m] = sb([P, S], F32, "d_sb%d" % m)
+                nc.scalar.copy(d_sb[m][:], d_accs[m][:])
+            for m in tiles:
+                e_pass(e_accs[m], m, 1)
+                res = sb([P, S], F32, "res%d" % m)
+                nc.vector.tensor_tensor(res[:], e_accs[m][:], d_sb[m][:], MULT)
+                nc.sync.dma_start(out[m * P : (m + 1) * P, :], res[:])

@@ -73,9 +73,15 @@ def tile_list_repository_matrix_kernel(
         rows = sb([P, 32], F32, "rows")
         win_a = sb([P, T], U8, "win_a")
         win_b = sb([P, T], U8, "win_b")
+
+        def clear(words):
+            cut = words.shape[1] // 2 + 1
+            nc.vector.memset(words[:, 0:cut], 0)
+            nc.vector.memset(words[:, cut:], 0)
+
+        nc.gpsimd.memset(rows[:], 0.0)
         nc.gpsimd.memset(win_b[:].bitcast(I32), 0)
-        nc.vector.memset(rows[:], 0.0)
-        nc.vector.memset(win_a[:].bitcast(I32), 0)
+        clear(win_a[:].bitcast(I32))
 
         def load_vector(n, vec):
             nc.sync.dma_start(
@@ -92,9 +98,9 @@ def tile_list_repository_matrix_kernel(
         w8s_raw = sb([P, H // 4], I32, "w8s_raw")
         planes_first = sb([P, W4S + SW], I32, "planes_first")
         planes_later = sb([P, 2 * S], U8, "planes_later")
-        nc.vector.memset(w8s_raw[:], 0)
-        nc.vector.memset(planes_first[:], 0)
-        nc.vector.memset(planes_later[:].bitcast(I32), 0)
+        clear(w8s_raw[:])
+        clear(planes_first[:])
+        clear(planes_later[:].bitcast(I32))
 
         def load_tab(a, tab):
             nc.sync.dma_start(tab[:], tab_words[a].rearrange("p t i -> p (t i)").bitcast(I32))

@@ -15,7 +15,6 @@ FP8X4 = mybir.dt.float8_e4m3fn_x4
 FP4X4 = mybir.dt.float4_e2m1fn_x4
 MULT = mybir.AluOpType.mult
 ADD = mybir.AluOpType.add
-IDENTITY = mybir.ActivationFunctionType.Identity
 COPY = mybir.ActivationFunctionType.Copy
 SIGMOID = mybir.ActivationFunctionType.Sigmoid
 
@@ -27,14 +26,16 @@ CT = H // P
 GROUPS = 16
 RUN = 8
 MT = S // P
-SCALAR_GAINS = 2
+POOL_COLS = 384
 EARLY = 6
 AT_TAB1 = 0
 AT_TAB2 = AT_TAB1 + 4 * T
 AT_W8_LO = AT_TAB2 + 4 * T + H
 AT_STAGED = AT_W8_LO + 9 * H
 AT_W8_HI = AT_STAGED + 4 * H
-AT_HALF = AT_W8_HI + 4 * H
+WOVEN = 2 * PACK * S
+AT_H_FLAT = AT_W8_HI + 4 * H
+AT_HQ = AT_H_FLAT + 5 * WOVEN // 2
 W4S = KP * H // 4
 SW = S // 4
 
@@ -165,10 +166,10 @@ def tile_list_repository_matrix_kernel(
         order_w4(2)
 
         w8_all = w8_words.rearrange("a p n i -> p a (n i)").bitcast(I32)
-        w8_lo = placed([P, 2, H], I32, "w8_lo", AT_W8_LO)
-        nc.sync.dma_start(w8_lo[:], w8_all[:, 0:2, :])
-        w8_hi = placed([P, 1, H], I32, "w8_hi", AT_W8_HI)
-        nc.sync.dma_start(w8_hi[:], w8_all[:, 2:3, :])
+        w8_raw = []
+        for a, at in enumerate((AT_W8_LO, AT_W8_LO + 4 * H, AT_W8_HI)):
+            w8_raw.append(placed([P, H], I32, "w8_raw%d" % a, at))
+            nc.sync.dma_start(w8_raw[a][:], w8_all[:, a, :])
         vs.append(gather_words(1))
         vs.append(gather_words(2))
         w4s_1hi = placed([P, (CT - EARLY) * 32], I32, "w4s_1hi", AT_TAB2)
@@ -184,16 +185,24 @@ def tile_list_repository_matrix_kernel(
         vecs = sb([P, CT, 4], F32, "vecs")
         nc.vector.transpose(vecs[:].rearrange("p c v -> p (c v)"), rows[:])
 
+        bias = sb([P, RP, PACK], F32, "bias")
+        bias_last = [placed([P, PACK], F32, "bias_last%d" % k, AT_HQ + k * 4 * S) for k in range(RP)]
+        nc.vector.tensor_copy(bias[:].rearrange("p k t -> p (k t)"), vecs[:, :, 2])
+        for k in range(RP):
+            nc.vector.tensor_copy(bias_last[k][:], vecs[:, PACK * k : PACK * (k + 1), 2])
+
         def load_docs(a, raw):
             nc.sync.dma_start(raw[:], docs[512 * a : 512 * (a + 1), :].rearrange("(p j) w -> p j w", j=PACK))
             return raw
 
         docs_raw = [load_docs(0, placed([P, PACK, S], F32, "docs0", AT_TAB1))]
 
-        def v_scale(a, lo, hi):
+        def v_scale(a, cols):
             if a == 0:
-                return planes_first[:, W4S : W4S + SW].bitcast(U8)[:, lo:hi]
-            return planes_later[:, (a - 1) * S + lo : (a - 1) * S + hi]
+                return planes_first[:, W4S : W4S + SW].bitcast(U8)[:, cols]
+            return planes_later[:, (a - 1) * S + cols.start : (a - 1) * S + cols.stop]
+
+        everything = slice(0, S)
 
         def a_pass(acc, c, a):
             nc.tensor.matmul_mx(
@@ -201,7 +210,7 @@ def tile_list_repository_matrix_kernel(
                 lhsT=w4[a][:, c * 64 : (c + 1) * 64].bitcast(FP4X4),
                 lhsT_scale=w4_plane(a, c),
                 rhs=vs[a][:].bitcast(FP8X4),
-                rhs_scale=v_scale(a, 0, S),
+                rhs_scale=v_scale(a, everything),
                 start=(a == 0),
                 stop=(a == KP - 1),
             )
@@ -215,152 +224,148 @@ def tile_list_repository_matrix_kernel(
                 a_pass(accs[c], c, a)
             nc.scalar.activation(sig[c // PACK][:, c % PACK, :], accs[c][:], SIGMOID, bias=vecs[:, c, 0:1])
 
-        w8 = []
-        for a in range(KP):
-            w = sb([P, H], I32, "w8_%d" % a)
-            if a < 2:
-                permute(w[:], w8_lo[:, a, :], 8)
-            else:
-                w8s = placed([P, H // 4], I32, "w8s", AT_W8_LO)
-                permute(w8s[:], w8s_raw[:], 2)
-                permute(w[:, 0 : H // 2], w8_hi[:, 0, :], 8, slice(0, PACK))
-                permute(w[:, H // 2 : H], w8_hi[:, 0, :], 8, slice(PACK, CT))
-            w8.append(w)
-        docs_raw.append(load_docs(1, placed([P, PACK, S], F32, "docs1", AT_TAB2 + H)))
-        docs_raw.append(load_docs(2, placed([P, PACK, S], F32, "docs2", AT_W8_LO + H)))
+        def weave(copy, woven, flat, run):
+            copy(woven.rearrange("p (n i) t -> p n t i", i=run), flat.rearrange("p t (n i) -> p n t i", i=run))
 
-        def quantized(name):
-            return sb([P, S], I32, name + "_codes"), sb([P, S], U8, name + "_plane")
+        def pool_cast(woven, raw):
+            nc.gpsimd.tensor_scalar(woven, raw.rearrange("p t n -> p n t"), 1.0, 0.0, MULT, ADD)
 
-        def quantize(dst, woven, cols):
+        def quantized(name, at=None):
+            codes = sb([P, S], I32, name + "_codes") if at is None else placed([P, S], I32, name + "_codes", at)
+            return codes, sb([P, S], U8, name + "_plane")
+
+        def quantize(dst, woven, cols=everything):
             nc.vector.quantize_mx(
                 dst[0][:, cols].bitcast(FP8X4), dst[1][:, cols], woven[:, cols, :].rearrange("p n t -> p (n t)")
             )
 
-        everything = slice(0, S)
+        h_flat = [placed([P, PACK, S], BF16, "h_flat0", AT_H_FLAT + WOVEN // 2), sb([P, PACK, S], BF16, "h_flat1")]
+        h_woven = [sb([P, S, PACK], BF16, "h_woven%d" % k) for k in range(RP)]
+        b_woven = []
+        w8 = [sb([P, H], I32, "w8_%d" % a) for a in range(KP)]
+        permute(w8[0][:], w8_raw[0][:], 8)
+        w8s = placed([P, H // 4], I32, "w8s", AT_W8_LO)
+        permute(w8s[:], w8s_raw[:], 2)
+        permute(w8[1][:], w8_raw[1][:], 8)
+        permute(w8[2][:], w8_raw[2][:], 8)
+        docs_raw.append(load_docs(1, placed([P, PACK, S], F32, "docs1", AT_TAB2 + H)))
+        docs_raw.append(load_docs(2, placed([P, PACK, S], F32, "docs2", AT_W8_LO + H)))
+        for t in range(PACK):
+            nc.vector.tensor_scalar_mul(h_flat[0][:, t, :], sig[0][:, t, :], vecs[:, t, 1:2])
+        weave(nc.vector.tensor_copy, h_woven[0][:], h_flat[0][:], 4)
 
-        def b_pass(acc, c, a, cols, start, stop):
+        def b_pass(acc, c, a, n, start, stop):
+            cols = slice(n * P, (n + 1) * P)
             nc.tensor.matmul_mx(
                 acc,
                 lhsT=w8[a][:, c * P : (c + 1) * P].bitcast(FP8X4),
                 lhsT_scale=w8s[:].bitcast(U8)[4 * a : P, c * P : (c + 1) * P],
                 rhs=vs[a][:, cols].bitcast(FP8X4),
-                rhs_scale=v_scale(a, cols.start, cols.stop),
+                rhs_scale=v_scale(a, cols),
                 start=start,
                 stop=stop,
             )
 
-        def weave(copy, woven, flat, run):
-            copy(woven.rearrange("p (n i) t -> p n t i", i=run), flat.rearrange("p t (n i) -> p n t i", i=run))
+        def b_sums(k, order):
+            sums = [bank(PACK * k + n, [P, PACK, P], "b%d_%d" % (k, n)) for n in range(MT)]
+            for a, n in order:
+                for t in range(PACK):
+                    b_pass(sums[n][:, t, :], PACK * k + t, a, n, (a, t) == (0, 0), (a, t) == (KP - 1, PACK - 1))
+            return sums
 
-        b_woven = [sb([P, S, PACK], BF16, "b_woven%d" % k) for k in range(RP)]
-        h_woven = [sb([P, S, PACK], BF16, "h_woven%d" % k) for k in range(RP)]
-        d_woven = [sb([P, S, PACK], BF16, "d_woven%d" % a) for a in range(KP - 1)]
-        h_flat = [sb([P, PACK, S], BF16, "h_flat%d" % k) for k in range(RP)]
-        b_flat = sb([P, PACK, S], BF16, "b_flat")
+        def b_reads(k, sums):
+            b_woven.append(placed([P, S, PACK], BF16, "b_woven%d" % k, AT_H_FLAT + WOVEN // (k + 1)))
+            for n in range(MT):
+                row = bias_last[k][:] if n == MT - 1 else bias[:, k, :]
+                nc.vector.tensor_tensor(
+                    b_woven[k][:, n * P : (n + 1) * P, :],
+                    sums[n][:].rearrange("p t n -> p n t"),
+                    row.unsqueeze(1).to_broadcast([P, P, PACK]),
+                    ADD,
+                )
+
+        pool_part, scalar_part = slice(0, POOL_COLS), slice(POOL_COLS, S)
         bq = [quantized("b%d" % k) for k in range(RP)]
         dq = [quantized("d%d" % a) for a in range(KP)]
-        hq = [quantized("h%d" % k) for k in range(RP)]
-        halves = [slice(0, S // 2), slice(S // 2, S)]
 
-        def quantize_half(dst, woven, cols):
-            nc.vector.quantize_mx(dst[0][:, cols].bitcast(FP8X4), dst[1][:, cols], woven[:].rearrange("p n t -> p (n t)"))
+        sums = b_sums(0, [(a, n) for n in range(MT) for a in range(KP)])
+        d_woven = [placed([P, S, PACK], BF16, "d_woven0", AT_H_FLAT)]
+        pool_cast(d_woven[0][:, pool_part, :], docs_raw[0][:, :, pool_part])
+        b_reads(0, sums)
+        weave(nc.scalar.copy, d_woven[0][:, scalar_part, :], docs_raw[0][:, :, scalar_part], 2)
 
-        def scale_h(k, tiles):
-            for t in tiles:
-                nc.vector.tensor_scalar_mul(h_flat[k][:, t, :], sig[k][:, t, :], vecs[:, PACK * k + t, 1:2])
-
-        bias_first = placed([P, PACK], F32, "bias_first", AT_HALF)
-        bias_later = sb([P, PACK], F32, "bias_later")
-        nc.vector.tensor_copy(bias_first[:], vecs[:, 0:PACK, 2])
-        nc.vector.tensor_copy(bias_later[:], vecs[:, 0:PACK, 2])
-        sums = [bank(n, [P, PACK, P], "b0_%d" % n) for n in range(MT)]
-        for a in range(KP):
-            for n in range(MT):
-                for t in range(PACK):
-                    first, last = (a, t) == (0, 0), (a, t) == (KP - 1, PACK - 1)
-                    b_pass(sums[n][:, t, :], t, a, slice(n * P, (n + 1) * P), first, last)
-        for n in range(MT):
-            nc.vector.tensor_tensor(
-                b_woven[0][:, n * P : (n + 1) * P, :],
-                sums[n][:].rearrange("p t n -> p n t"),
-                (bias_later if n else bias_first)[:].unsqueeze(1).to_broadcast([P, P, PACK]),
-                ADD,
-            )
-
-        first_woven = [placed([P, S // 2, PACK], BF16, "d_first0", AT_HALF), sb([P, S // 2, PACK], BF16, "d_first1")]
-        nc.gpsimd.tensor_scalar(
-            first_woven[0][:], docs_raw[0][:, :, halves[0]].rearrange("p t n -> p n t"), 1.0, 0.0, MULT, ADD
-        )
-        weave(nc.scalar.copy, first_woven[1][:], docs_raw[0][:, :, halves[1]], 2)
-        for t in range(PACK - SCALAR_GAINS, PACK):
+        def scalar_gain(t):
             nc.scalar.activation(h_flat[1][:, t, :], sig[1][:, t, :], COPY, scale=vecs[:, PACK + t, 1:2])
-        weave(nc.scalar.copy, d_woven[0][:], docs_raw[1][:], 2)
-        for t in range(PACK):
-            acc = bank(PACK + t, [P, S], "b%d" % t)
-            for a in range(KP):
-                b_pass(acc[:], PACK + t, a, everything, a == 0, a == KP - 1)
-            nc.scalar.activation(b_flat[:, t, :], acc[:], IDENTITY, bias=vecs[:, PACK + t, 2:3])
-        for cols in halves:
-            weave(nc.scalar.copy, d_woven[1][:, cols, :], docs_raw[2][:, :, cols], 2)
 
-        scale_h(0, range(PACK))
-        weave(nc.vector.tensor_copy, h_woven[0][:], h_flat[0][:], 4)
-        quantize(bq[0], b_woven[0], everything)
-        quantize_half(dq[0], first_woven[1], halves[1])
-        quantize_half(dq[0], first_woven[0], halves[0])
-        quantize(dq[1], d_woven[0], everything)
-        quantize(hq[0], h_woven[0], everything)
-        weave(nc.vector.tensor_copy, b_woven[1][:], b_flat[:], 4)
-        quantize(dq[2], d_woven[1], halves[0])
-        quantize(bq[1], b_woven[1], everything)
-        quantize(dq[2], d_woven[1], halves[1])
-        scale_h(1, range(PACK - SCALAR_GAINS))
+        scalar_gain(0)
+        scalar_gain(1)
+        d_woven.append(sb([P, S, PACK], BF16, "d_woven1"))
+        weave(nc.scalar.copy, d_woven[1][:], docs_raw[1][:], 2)
+        scalar_gain(2)
+        scalar_gain(3)
+        sums = b_sums(1, [(a, n) for n in range(MT) for a in range(KP)])
+        hq = [quantized("h0", AT_HQ)]
+        quantize(dq[0], d_woven[0])
+        quantize(hq[0], h_woven[0])
+        quantize(bq[0], b_woven[0])
+        d_woven.append(placed([P, S, PACK], BF16, "d_woven2", AT_H_FLAT + 3 * WOVEN // 2))
+        pool_cast(d_woven[2][:, pool_part, :], docs_raw[2][:, :, pool_part])
+        b_reads(1, sums)
+        weave(nc.scalar.copy, d_woven[2][:, scalar_part, :], docs_raw[2][:, :, scalar_part], 2)
+        halves = [slice(0, S // 2), slice(S // 2, S)]
         for cols in halves:
-            weave(nc.vector.tensor_copy, h_woven[1][:, cols, :], h_flat[1][:, :, cols], 4)
-        for cols in halves:
-            quantize(hq[1], h_woven[1], cols)
+            weave(nc.scalar.copy, h_woven[1][:, cols, :], h_flat[1][:, :, cols], 4)
+        hq.append(quantized("h1"))
+        dq[1] = placed([P, S], I32, "d1_codes", AT_HQ + 4 * S), dq[1][1]
+        for a in range(1, KP):
+            quantize(dq[a], d_woven[a], halves[0])
+        quantize(bq[1], b_woven[1])
+        quantize(hq[1], h_woven[1])
+        for a in range(1, KP):
+            quantize(dq[a], d_woven[a], halves[1])
 
-        def d_pass(acc, m, a, start, stop):
+        def last_pass(acc, m, left, right, right_scale, start, stop):
             cols = slice(m * P, (m + 1) * P)
             nc.tensor.matmul_mx(
                 acc[:],
-                lhsT=dq[a][0][:, cols].bitcast(FP8X4),
-                lhsT_scale=dq[a][1][:, cols],
-                rhs=vs[a][:].bitcast(FP8X4),
-                rhs_scale=v_scale(a, 0, S),
+                lhsT=left[0][:, cols].bitcast(FP8X4),
+                lhsT_scale=left[1][:, cols],
+                rhs=right.bitcast(FP8X4),
+                rhs_scale=right_scale,
                 start=start,
                 stop=stop,
             )
 
-        def e_pass(acc, m, k):
-            cols = slice(m * P, (m + 1) * P)
-            nc.tensor.matmul_mx(
-                acc[:],
-                lhsT=hq[k][0][:, cols].bitcast(FP8X4),
-                lhsT_scale=hq[k][1][:, cols],
-                rhs=bq[k][0][:].bitcast(FP8X4),
-                rhs_scale=bq[k][1][:],
-                start=(k == 0),
-                stop=(k == RP - 1),
-            )
+        def d_pass(m, a):
+            last_pass(d_accs[m], m, dq[a], vs[a][:], v_scale(a, everything), a == 0, a == KP - 1)
+
+        def e_pass(m, k):
+            last_pass(e_accs[m], m, hq[k], bq[k][0][:], bq[k][1][:], k == 0, k == RP - 1)
 
         d_accs = [bank(m, [P, S], "d%d" % m) for m in range(MT)]
         e_accs = [bank(PACK + m, [P, S], "e%d" % m) for m in range(MT)]
-        for a in range(KP - 1):
-            for m in range(MT):
-                d_pass(d_accs[m], m, a, a == 0, False)
         for m in range(MT):
-            e_pass(e_accs[m], m, 0)
-        for pair in range(MT // 2):
-            tiles = (2 * pair, 2 * pair + 1)
-            d_sb = {}
-            for m in tiles:
-                d_pass(d_accs[m], m, 2, False, True)
-                d_sb[m] = sb([P, S], F32, "d_sb%d" % m)
-                nc.scalar.copy(d_sb[m][:], d_accs[m][:])
-            for m in tiles:
-                e_pass(e_accs[m], m, 1)
-                res = sb([P, S], F32, "res%d" % m)
-                nc.vector.tensor_tensor(res[:], e_accs[m][:], d_sb[m][:], MULT)
-                nc.sync.dma_start(out[m * P : (m + 1) * P, :], res[:])
+            d_pass(m, 0)
+        for m in range(MT):
+            e_pass(m, 0)
+        kept = [sb([P, S], F32, "kept%d" % m) for m in range(MT)]
+
+        def finish(m, acc):
+            res = sb([P, S], F32, "res%d" % m)
+            nc.vector.tensor_tensor(res[:], acc[:], kept[m][:], MULT)
+            nc.sync.dma_start(out[m * P : (m + 1) * P, :], res[:])
+
+        for m in range(MT // 2):
+            for a in range(1, KP):
+                d_pass(m, a)
+            nc.scalar.copy(kept[m][:], d_accs[m][:])
+        for m in range(MT):
+            e_pass(m, 1)
+            if m < MT // 2:
+                finish(m, e_accs[m])
+            else:
+                nc.scalar.copy(kept[m][:], e_accs[m][:])
+        for m in range(MT // 2, MT):
+            for a in range(1, KP):
+                d_pass(m, a)
+            finish(m, d_accs[m])

@@ -81,8 +81,8 @@ def tile_list_repository_matrix_kernel(
             nc.vector.memset(words[:, cut:], 0)
 
         nc.gpsimd.memset(rows[:], 0.0)
-        nc.gpsimd.memset(win_b[:].bitcast(I32), 0)
-        clear(win_a[:].bitcast(I32))
+        nc.gpsimd.memset(win_a[:].bitcast(I32), 0)
+        nc.vector.memset(win_b[:].bitcast(I32), 0)
 
         def load_vector(n, vec):
             nc.sync.dma_start(
@@ -112,7 +112,7 @@ def tile_list_repository_matrix_kernel(
         nc.sync.dma_start(w4_later[:], w4_all[1:KP].rearrange("a p n -> p a n"))
         load_vector(2, b2)
         for d in range(4):
-            nc.gpsimd.dma_start(w8s_raw[32 * d : 32 * d + 4 * KP, :], w8_scales.bitcast(I32)[:, 4 * d : 4 * d + 4, :])
+            nc.gpsimd.dma_start(w8s_raw[32 * d + 4 : 32 * d + 4 * (KP + 1), :], w8_scales.bitcast(I32)[:, 4 * d : 4 * d + 4, :])
 
         pick_a = placed([P, S], U8, "pick_a", AT_TAB1)
         nc.vector.tensor_copy(pick_a[:], win_a[:].indirect(offsets[:]))
@@ -259,7 +259,7 @@ def tile_list_repository_matrix_kernel(
             nc.tensor.matmul_mx(
                 acc,
                 lhsT=w8[a][:, c * P : (c + 1) * P].bitcast(FP8X4),
-                lhsT_scale=w8s[:].bitcast(U8)[4 * a : P, c * P : (c + 1) * P],
+                lhsT_scale=w8s[:].bitcast(U8)[4 * (a + 1) : P, c * P : (c + 1) * P],
                 rhs=vs[a][:, cols].bitcast(FP8X4),
                 rhs_scale=v_scale(a, cols),
                 start=start,

@@ -15,7 +15,6 @@ FP8X4 = mybir.dt.float8_e4m3fn_x4
 FP4X4 = mybir.dt.float4_e2m1fn_x4
 MULT = mybir.AluOpType.mult
 ADD = mybir.AluOpType.add
-COPY = mybir.ActivationFunctionType.Copy
 SIGMOID = mybir.ActivationFunctionType.Sigmoid
 
 P = 128
@@ -29,13 +28,15 @@ MT = S // P
 POOL_COLS = 384
 EARLY = 6
 AT_TAB1 = 0
-AT_TAB2 = AT_TAB1 + 4 * T
-AT_W8_LO = AT_TAB2 + 4 * T + H
+AT_DOCS0 = AT_TAB1 + H
+AT_TAB2 = AT_DOCS0 + 4 * T
+AT_W8_LO = AT_TAB2 + 4 * T
 AT_STAGED = AT_W8_LO + 9 * H
 AT_W8_HI = AT_STAGED + 4 * H
 WOVEN = 2 * PACK * S
 AT_H_FLAT = AT_W8_HI + 4 * H
-AT_HQ = AT_H_FLAT + 5 * WOVEN // 2
+AT_HQ = AT_H_FLAT + 2 * WOVEN
+AT_SIG = AT_HQ + 2 * WOVEN
 W4S = KP * H // 4
 SW = S // 4
 
@@ -158,9 +159,7 @@ def tile_list_repository_matrix_kernel(
         order_w4(0)
         vs = [gather_words(0)]
         order_w4_scales(0)
-        w4s_1lo = sb([P, EARLY * 32], I32, "w4s_1lo")
-        permute(w4s_1lo[:], planes_first[:, H // 4 : H // 2], 2, slice(0, EARLY))
-        w4s.append(None)
+        order_w4_scales(1)
         order_w4_scales(2)
         order_w4(1)
         order_w4(2)
@@ -172,21 +171,15 @@ def tile_list_repository_matrix_kernel(
             nc.sync.dma_start(w8_raw[a][:], w8_all[:, a, :])
         vs.append(gather_words(1))
         vs.append(gather_words(2))
-        w4s_1hi = placed([P, (CT - EARLY) * 32], I32, "w4s_1hi", AT_TAB2)
-        permute(w4s_1hi[:], planes_first[:, H // 4 : H // 2], 2, slice(EARLY, CT))
 
         def w4_plane(a, c):
-            if a == 1 and c < EARLY:
-                return w4s_1lo[:].bitcast(U8)[:, c * P : (c + 1) * P]
-            if a == 1:
-                return w4s_1hi[:].bitcast(U8)[:, (c - EARLY) * P : (c - EARLY + 1) * P]
             return w4s[a][:].bitcast(U8)[:, c * P : (c + 1) * P]
 
         vecs = sb([P, CT, 4], F32, "vecs")
         nc.vector.transpose(vecs[:].rearrange("p c v -> p (c v)"), rows[:])
 
         bias = sb([P, RP, PACK], F32, "bias")
-        bias_last = [placed([P, PACK], F32, "bias_last%d" % k, AT_HQ + k * 4 * S) for k in range(RP)]
+        bias_last = [placed([P, PACK], F32, "bias_last%d" % k, AT_HQ + k * 8 * S) for k in range(RP)]
         nc.vector.tensor_copy(bias[:].rearrange("p k t -> p (k t)"), vecs[:, :, 2])
         for k in range(RP):
             nc.vector.tensor_copy(bias_last[k][:], vecs[:, PACK * k : PACK * (k + 1), 2])
@@ -195,7 +188,7 @@ def tile_list_repository_matrix_kernel(
             nc.sync.dma_start(raw[:], docs[512 * a : 512 * (a + 1), :].rearrange("(p j) w -> p j w", j=PACK))
             return raw
 
-        docs_raw = [load_docs(0, placed([P, PACK, S], F32, "docs0", AT_TAB1))]
+        docs_raw = [load_docs(0, placed([P, PACK, S], F32, "docs0", AT_DOCS0))]
 
         def v_scale(a, cols):
             if a == 0:
@@ -204,7 +197,7 @@ def tile_list_repository_matrix_kernel(
 
         everything = slice(0, S)
 
-        def a_pass(acc, c, a):
+        def a_pass(acc, c, a, stop):
             nc.tensor.matmul_mx(
                 acc[:],
                 lhsT=w4[a][:, c * 64 : (c + 1) * 64].bitcast(FP4X4),
@@ -212,16 +205,17 @@ def tile_list_repository_matrix_kernel(
                 rhs=vs[a][:].bitcast(FP8X4),
                 rhs_scale=v_scale(a, everything),
                 start=(a == 0),
-                stop=(a == KP - 1),
+                stop=stop,
             )
 
-        sig = [sb([P, PACK, S], F32, "sig%d" % k) for k in range(RP)]
+        sig = [placed([P, PACK, S], F32, "sig0", AT_SIG), sb([P, PACK, S], F32, "sig1")]
         accs = [bank(c, [P, S], "a%d" % c) for c in range(CT)]
         for c in range(CT):
-            a_pass(accs[c], c, 0)
+            a_pass(accs[c], c, 0, False)
         for c in range(CT):
-            for a in range(1, KP):
-                a_pass(accs[c], c, a)
+            later = (1, 2) if c < EARLY else (2, 1)
+            for a in later:
+                a_pass(accs[c], c, a, a == later[-1])
             nc.scalar.activation(sig[c // PACK][:, c % PACK, :], accs[c][:], SIGMOID, bias=vecs[:, c, 0:1])
 
         def weave(copy, woven, flat, run):
@@ -239,20 +233,20 @@ def tile_list_repository_matrix_kernel(
                 dst[0][:, cols].bitcast(FP8X4), dst[1][:, cols], woven[:, cols, :].rearrange("p n t -> p (n t)")
             )
 
-        h_flat = [placed([P, PACK, S], BF16, "h_flat0", AT_H_FLAT + WOVEN // 2), sb([P, PACK, S], BF16, "h_flat1")]
-        h_woven = [sb([P, S, PACK], BF16, "h_woven%d" % k) for k in range(RP)]
+        h_flat = [placed([P, PACK, S], BF16, "h_flat0", AT_H_FLAT + WOVEN // 2)]
+        h_first = sb([P, S, PACK], BF16, "h_first")
         b_woven = []
         w8 = [sb([P, H], I32, "w8_%d" % a) for a in range(KP)]
-        permute(w8[0][:], w8_raw[0][:], 8)
-        w8s = placed([P, H // 4], I32, "w8s", AT_W8_LO)
+        w8s = placed([P, H // 4], I32, "w8s", AT_TAB1)
         permute(w8s[:], w8s_raw[:], 2)
+        permute(w8[0][:], w8_raw[0][:], 8)
         permute(w8[1][:], w8_raw[1][:], 8)
         permute(w8[2][:], w8_raw[2][:], 8)
-        docs_raw.append(load_docs(1, placed([P, PACK, S], F32, "docs1", AT_TAB2 + H)))
+        docs_raw.append(load_docs(1, placed([P, PACK, S], F32, "docs1", AT_TAB2)))
         docs_raw.append(load_docs(2, placed([P, PACK, S], F32, "docs2", AT_W8_LO + H)))
         for t in range(PACK):
             nc.vector.tensor_scalar_mul(h_flat[0][:, t, :], sig[0][:, t, :], vecs[:, t, 1:2])
-        weave(nc.vector.tensor_copy, h_woven[0][:], h_flat[0][:], 4)
+        weave(nc.vector.tensor_copy, h_first[:], h_flat[0][:], 4)
 
         def b_pass(acc, c, a, n, start, stop):
             cols = slice(n * P, (n + 1) * P)
@@ -274,9 +268,9 @@ def tile_list_repository_matrix_kernel(
             return sums
 
         def b_reads(k, sums):
-            b_woven.append(placed([P, S, PACK], BF16, "b_woven%d" % k, AT_H_FLAT + WOVEN // (k + 1)))
+            b_woven.append(placed([P, S, PACK], BF16, "b_woven%d" % k, AT_SIG + (3 - k) * WOVEN // 2))
             for n in range(MT):
-                row = bias_last[k][:] if n == MT - 1 else bias[:, k, :]
+                row = bias_last[k][:] if n == MT - 2 else bias[:, k, :]
                 nc.vector.tensor_tensor(
                     b_woven[k][:, n * P : (n + 1) * P, :],
                     sums[n][:].rearrange("p t n -> p n t"),
@@ -286,41 +280,37 @@ def tile_list_repository_matrix_kernel(
 
         pool_part, scalar_part = slice(0, POOL_COLS), slice(POOL_COLS, S)
         bq = [quantized("b%d" % k) for k in range(RP)]
-        dq = [quantized("d%d" % a) for a in range(KP)]
 
         sums = b_sums(0, [(a, n) for n in range(MT) for a in range(KP)])
-        d_woven = [placed([P, S, PACK], BF16, "d_woven0", AT_H_FLAT)]
-        pool_cast(d_woven[0][:, pool_part, :], docs_raw[0][:, :, pool_part])
+        h_flat.append(placed([P, PACK, S], BF16, "h_flat1", AT_H_FLAT))
+        for t in range(PACK):
+            nc.gpsimd.tensor_scalar(h_flat[1][:, t, :], sig[1][:, t, :], vecs[:, PACK + t, 1:2], 0.0, MULT, ADD)
         b_reads(0, sums)
-        weave(nc.scalar.copy, d_woven[0][:, scalar_part, :], docs_raw[0][:, :, scalar_part], 2)
-
-        def scalar_gain(t):
-            nc.scalar.activation(h_flat[1][:, t, :], sig[1][:, t, :], COPY, scale=vecs[:, PACK + t, 1:2])
-
-        scalar_gain(0)
-        scalar_gain(1)
-        d_woven.append(sb([P, S, PACK], BF16, "d_woven1"))
-        weave(nc.scalar.copy, d_woven[1][:], docs_raw[1][:], 2)
-        scalar_gain(2)
-        scalar_gain(3)
-        sums = b_sums(1, [(a, n) for n in range(MT) for a in range(KP)])
-        hq = [quantized("h0", AT_HQ)]
-        quantize(dq[0], d_woven[0])
-        quantize(hq[0], h_woven[0])
-        quantize(bq[0], b_woven[0])
-        d_woven.append(placed([P, S, PACK], BF16, "d_woven2", AT_H_FLAT + 3 * WOVEN // 2))
-        pool_cast(d_woven[2][:, pool_part, :], docs_raw[2][:, :, pool_part])
-        b_reads(1, sums)
-        weave(nc.scalar.copy, d_woven[2][:, scalar_part, :], docs_raw[2][:, :, scalar_part], 2)
+        d_first = placed([P, S, PACK], BF16, "d_first", AT_SIG + 5 * WOVEN // 2)
+        weave(nc.scalar.copy, d_first[:], docs_raw[0][:], 2)
         halves = [slice(0, S // 2), slice(S // 2, S)]
-        for cols in halves:
-            weave(nc.scalar.copy, h_woven[1][:, cols, :], h_flat[1][:, :, cols], 4)
-        hq.append(quantized("h1"))
-        dq[1] = placed([P, S], I32, "d1_codes", AT_HQ + 4 * S), dq[1][1]
+        d_woven = {a: sb([P, S, PACK], BF16, "d_woven%d" % a) for a in range(1, KP)}
+        for a in range(1, KP):
+            weave(nc.scalar.copy, d_woven[a][:, halves[0], :], docs_raw[a][:, :, halves[0]], 2)
+        sums = b_sums(1, [(a, n) for n in range(MT) for a in range(KP)])
+        first_codes = placed([P, 2 * S], I32, "first_codes", AT_HQ)
+        hq = [(first_codes[:, 0:S], sb([P, S], U8, "h0_plane")), quantized("h1")]
+        dq = [(first_codes[:, S : 2 * S], sb([P, S], U8, "d0_plane"))]
+        quantize(hq[0], h_first)
+        quantize(bq[0], b_woven[0])
+        quantize(dq[0], d_first)
+        h_woven = placed([P, S, PACK], BF16, "h_woven", AT_SIG + 2 * WOVEN)
+        pool_cast(h_woven[:, pool_part, :], h_flat[1][:, :, pool_part])
+        b_reads(1, sums)
+        weave(nc.scalar.copy, h_woven[:, scalar_part, :], h_flat[1][:, :, scalar_part], 4)
+        for a in range(1, KP):
+            weave(nc.scalar.copy, d_woven[a][:, halves[1], :], docs_raw[a][:, :, halves[1]], 2)
+        d_codes = placed([P, 2 * S], I32, "d_codes", AT_HQ + 8 * S)
+        dq.extend((d_codes[:, (a - 1) * S : a * S], sb([P, S], U8, "d%d_plane" % a)) for a in range(1, KP))
         for a in range(1, KP):
             quantize(dq[a], d_woven[a], halves[0])
         quantize(bq[1], b_woven[1])
-        quantize(hq[1], h_woven[1])
+        quantize(hq[1], h_woven)
         for a in range(1, KP):
             quantize(dq[a], d_woven[a], halves[1])
 

@@ -15,6 +15,7 @@ FP8X4 = mybir.dt.float8_e4m3fn_x4
 FP4X4 = mybir.dt.float4_e2m1fn_x4
 MULT = mybir.AluOpType.mult
 ADD = mybir.AluOpType.add
+COPY = mybir.ActivationFunctionType.Copy
 SIGMOID = mybir.ActivationFunctionType.Sigmoid
 
 P = 128
@@ -25,7 +26,8 @@ CT = H // P
 GROUPS = 16
 RUN = 8
 MT = S // P
-POOL_COLS = 384
+POOL_COLS = 352
+POOL_GAINS = 3
 EARLY = 6
 AT_TAB1 = 0
 AT_DOCS0 = AT_TAB1 + H
@@ -283,15 +285,16 @@ def tile_list_repository_matrix_kernel(
 
         sums = b_sums(0, [(a, n) for n in range(MT) for a in range(KP)])
         h_flat.append(placed([P, PACK, S], BF16, "h_flat1", AT_H_FLAT))
-        for t in range(PACK):
+        for t in range(POOL_GAINS):
             nc.gpsimd.tensor_scalar(h_flat[1][:, t, :], sig[1][:, t, :], vecs[:, PACK + t, 1:2], 0.0, MULT, ADD)
         b_reads(0, sums)
+        for t in range(POOL_GAINS, PACK):
+            nc.scalar.activation(h_flat[1][:, t, :], sig[1][:, t, :], COPY, scale=vecs[:, PACK + t, 1:2])
         d_first = placed([P, S, PACK], BF16, "d_first", AT_SIG + 5 * WOVEN // 2)
         weave(nc.scalar.copy, d_first[:], docs_raw[0][:], 2)
         halves = [slice(0, S // 2), slice(S // 2, S)]
         d_woven = {a: sb([P, S, PACK], BF16, "d_woven%d" % a) for a in range(1, KP)}
-        for a in range(1, KP):
-            weave(nc.scalar.copy, d_woven[a][:, halves[0], :], docs_raw[a][:, :, halves[0]], 2)
+        weave(nc.scalar.copy, d_woven[1][:], docs_raw[1][:], 2)
         sums = b_sums(1, [(a, n) for n in range(MT) for a in range(KP)])
         first_codes = placed([P, 2 * S], I32, "first_codes", AT_HQ)
         hq = [(first_codes[:, 0:S], sb([P, S], U8, "h0_plane")), quantized("h1")]
@@ -303,8 +306,8 @@ def tile_list_repository_matrix_kernel(
         pool_cast(h_woven[:, pool_part, :], h_flat[1][:, :, pool_part])
         b_reads(1, sums)
         weave(nc.scalar.copy, h_woven[:, scalar_part, :], h_flat[1][:, :, scalar_part], 4)
-        for a in range(1, KP):
-            weave(nc.scalar.copy, d_woven[a][:, halves[1], :], docs_raw[a][:, :, halves[1]], 2)
+        for cols in halves:
+            weave(nc.scalar.copy, d_woven[2][:, cols, :], docs_raw[2][:, :, cols], 2)
         d_codes = placed([P, 2 * S], I32, "d_codes", AT_HQ + 8 * S)
         dq.extend((d_codes[:, (a - 1) * S : a * S], sb([P, S], U8, "d%d_plane" % a)) for a in range(1, KP))
         for a in range(1, KP):

@@ -29,6 +29,7 @@ MT = S // P
 POOL_COLS = 352
 POOL_GAINS = 3
 EARLY = 6
+ORDER = (1, 0, 2)
 AT_TAB1 = 0
 AT_DOCS0 = AT_TAB1 + H
 AT_TAB2 = AT_DOCS0 + 4 * T
@@ -66,11 +67,10 @@ def tile_list_repository_matrix_kernel(
 
         w4_all = w4_words.bitcast(I32)
         w4_first = sb([P, H // 2], I32, "w4_first")
-        nc.sync.dma_start(w4_first[:], w4_all[0])
+        nc.sync.dma_start(w4_first[:], w4_all[ORDER[0]])
         staged = placed([P, W4S + SW], I32, "staged", AT_STAGED)
-        staged_later = sb([P, 2 * SW], I32, "staged_later")
         nc.sync.dma_start(
-            staged[0:P:8, 0:W4S].rearrange("q (a n) -> q a n", a=KP),
+            staged[4:P:8, 0:W4S].rearrange("q (a n) -> q a n", a=KP),
             w4_scales.bitcast(I32).rearrange("a q n -> q a n"),
         )
 
@@ -97,22 +97,21 @@ def tile_list_repository_matrix_kernel(
         load_vector(1, gain)
         tab_rows = tab_scales.bitcast(I32)
         nc.sync.dma_start(win_a[0:P:4, :].bitcast(I32), tab_rows[0:2].rearrange("a q n -> q a n"))
-        nc.sync.dma_start(win_b[4:P:8, :].bitcast(I32), tab_rows[2])
+        nc.sync.dma_start(win_b[0:P:8, :].bitcast(I32), tab_rows[2])
 
         w8s_raw = sb([P, H // 4], I32, "w8s_raw")
         planes_first = sb([P, W4S + SW], I32, "planes_first")
-        planes_later = sb([P, 2 * S], U8, "planes_later")
+        planes_later = sb([P, 2 * SW], I32, "planes_later")
         clear(w8s_raw[:])
         clear(planes_first[:])
-        clear(planes_later[:].bitcast(I32))
 
         def load_tab(a, tab):
-            nc.sync.dma_start(tab[:], tab_words[a].rearrange("p t i -> p (t i)").bitcast(I32))
+            nc.sync.dma_start(tab[:], tab_words[ORDER[a]].rearrange("p t i -> p (t i)").bitcast(I32))
             return tab
 
         tabs = [load_tab(0, placed([P, T], I32, "tab0", AT_W8_LO))]
         w4_later = placed([P, 2, H // 2], I32, "w4_later", AT_W8_HI)
-        nc.sync.dma_start(w4_later[:], w4_all[1:KP].rearrange("a p n -> p a n"))
+        nc.sync.dma_start(w4_later[:], w4_all[0:KP:2].rearrange("a p n -> p a n"))
         load_vector(2, b2)
         for d in range(4):
             nc.gpsimd.dma_start(w8s_raw[32 * d + 4 : 32 * d + 4 * (KP + 1), :], w8_scales.bitcast(I32)[:, 4 * d : 4 * d + 4, :])
@@ -120,15 +119,15 @@ def tile_list_repository_matrix_kernel(
         pick_a = placed([P, S], U8, "pick_a", AT_TAB1)
         nc.vector.tensor_copy(pick_a[:], win_a[:].indirect(offsets[:]))
         nc.vector.tensor_copy(staged[:, W4S : W4S + SW], pick_a[:].bitcast(I32))
-        nc.vector.tensor_copy(staged_later[:, 0:SW], pick_a[:].bitcast(I32))
+        nc.vector.tensor_copy(planes_later[:, 0:SW], pick_a[:].bitcast(I32))
         for r in range(4):
-            nc.sync.dma_start(planes_first[r:P:32, :], staged[8 * r : P : 32, :])
+            nc.sync.dma_start(planes_first[r:P:32, :], staged[8 * r + 4 : P : 32, :])
         tabs.append(load_tab(1, placed([P, T], I32, "tab1", AT_TAB1)))
         pick_b = placed([P, S], U8, "pick_b", AT_TAB2)
         nc.vector.tensor_copy(pick_b[:], win_b[:].indirect(offsets[:]))
-        nc.vector.tensor_copy(staged_later[:, SW : 2 * SW], pick_b[:].bitcast(I32))
-        for r in range(4):
-            nc.sync.dma_start(planes_later[r:P:32, :].bitcast(I32), staged_later[8 * r + 4 : P : 32, :])
+        nc.vector.tensor_copy(planes_later[:, SW : 2 * SW], pick_b[:].bitcast(I32))
+        for r in range(1, 4):
+            nc.sync.dma_start(planes_later[r:P:32, :], planes_later[8 * r : P : 32, :])
         tabs.append(load_tab(2, placed([P, T], I32, "tab2", AT_TAB2)))
 
         def permute(dst, src, words, tiles=slice(0, CT)):
@@ -155,7 +154,7 @@ def tile_list_repository_matrix_kernel(
 
         def order_w4_scales(a):
             ws = sb([P, H // 4], I32, "w4s_%d" % a)
-            permute(ws[:], planes_first[:, a * H // 4 : (a + 1) * H // 4], 2)
+            permute(ws[:], planes_first[:, ORDER[a] * H // 4 : (ORDER[a] + 1) * H // 4], 2)
             w4s.append(ws)
 
         order_w4(0)
@@ -170,7 +169,7 @@ def tile_list_repository_matrix_kernel(
         w8_raw = []
         for a, at in enumerate((AT_W8_LO, AT_W8_LO + 4 * H, AT_W8_HI)):
             w8_raw.append(placed([P, H], I32, "w8_raw%d" % a, at))
-            nc.sync.dma_start(w8_raw[a][:], w8_all[:, a, :])
+            nc.sync.dma_start(w8_raw[a][:], w8_all[:, ORDER[a], :])
         vs.append(gather_words(1))
         vs.append(gather_words(2))
 
@@ -187,7 +186,7 @@ def tile_list_repository_matrix_kernel(
             nc.vector.tensor_copy(bias_last[k][:], vecs[:, PACK * k : PACK * (k + 1), 2])
 
         def load_docs(a, raw):
-            nc.sync.dma_start(raw[:], docs[512 * a : 512 * (a + 1), :].rearrange("(p j) w -> p j w", j=PACK))
+            nc.sync.dma_start(raw[:], docs[512 * ORDER[a] : 512 * (ORDER[a] + 1), :].rearrange("(p j) w -> p j w", j=PACK))
             return raw
 
         docs_raw = [load_docs(0, placed([P, PACK, S], F32, "docs0", AT_DOCS0))]
@@ -195,7 +194,7 @@ def tile_list_repository_matrix_kernel(
         def v_scale(a, cols):
             if a == 0:
                 return planes_first[:, W4S : W4S + SW].bitcast(U8)[:, cols]
-            return planes_later[:, (a - 1) * S + cols.start : (a - 1) * S + cols.stop]
+            return planes_later[:].bitcast(U8)[:, (a - 1) * S + cols.start : (a - 1) * S + cols.stop]
 
         everything = slice(0, S)
 
@@ -255,7 +254,7 @@ def tile_list_repository_matrix_kernel(
             nc.tensor.matmul_mx(
                 acc,
                 lhsT=w8[a][:, c * P : (c + 1) * P].bitcast(FP8X4),
-                lhsT_scale=w8s[:].bitcast(U8)[4 * (a + 1) : P, c * P : (c + 1) * P],
+                lhsT_scale=w8s[:].bitcast(U8)[4 * (ORDER[a] + 1) : P, c * P : (c + 1) * P],
                 rhs=vs[a][:, cols].bitcast(FP8X4),
                 rhs_scale=v_scale(a, cols),
                 start=start,
@@ -344,9 +343,11 @@ def tile_list_repository_matrix_kernel(
         kept = [sb([P, S], F32, "kept%d" % m) for m in range(MT)]
 
         def finish(m, acc):
-            res = sb([P, S], F32, "res%d" % m)
-            nc.vector.tensor_tensor(res[:], acc[:], kept[m][:], MULT)
-            nc.sync.dma_start(out[m * P : (m + 1) * P, :], res[:])
+            cut = {0: P, MT - 1: S - P}.get(m)
+            for cols in [everything] if cut is None else [slice(0, cut), slice(cut, S)]:
+                res = sb([P, cols.stop - cols.start], F32, "res%d_%d" % (m, cols.start))
+                nc.vector.tensor_tensor(res[:], acc[:, cols], kept[m][:, cols], MULT)
+                nc.sync.dma_start(out[m * P : (m + 1) * P, cols], res[:])
 
         for m in range(MT // 2):
             for a in range(1, KP):

@@ -54,10 +54,10 @@ def tile_list_repository_matrix_kernel(
         psum = ctx.enter_context(tc.psum_pool(name="psum", bufs=1))
 
         def sb(shape, dtype, name, tag=None):
-            return keep.tile(shape, dtype, name=name, tag=tag or name, align_bytes=64)
+            return keep.tile(shape, dtype, name=name, tag=tag or name, align_bytes=256)
 
         def placed(shape, dtype, name, offset):
-            return shared.tile(shape, dtype, name=name, tag=name, align_bytes=64, offset=offset)
+            return shared.tile(shape, dtype, name=name, tag=name, align_bytes=256, offset=offset)
 
         def bank(n, shape, name):
             return psum.tile(shape, F32, name=name, tag="bank%d" % n)

from contextlib import ExitStack

import concourse.mybir as mybir

K, H, T, S = 1536, 1024, 2048, 512
FLOPS = 2 * K * H * S * 2 + 2 * K * S * S + 2 * H * S * S

F32 = mybir.dt.float32
BF16 = mybir.dt.bfloat16
I32 = mybir.dt.int32
U32 = mybir.dt.uint32
U16 = mybir.dt.uint16
U8 = mybir.dt.uint8
FP8X4 = mybir.dt.float8_e4m3fn_x4
FP4X4 = mybir.dt.float4_e2m1fn_x4
MULT = mybir.AluOpType.mult
ADD = mybir.AluOpType.add
COPY = mybir.ActivationFunctionType.Copy
SIGMOID = mybir.ActivationFunctionType.Sigmoid

P = 128
PACK = 4
KP = K // (P * PACK)
RP = H // (P * PACK)
CT = H // P
GROUPS = 16
RUN = 8
MT = S // P
POOL_COLS = 352
POOL_GAINS = 3
EARLY = 6
ORDER = (1, 0, 2)
AT_TAB1 = 0
AT_DOCS0 = AT_TAB1 + H
AT_TAB2 = AT_DOCS0 + 4 * T
AT_W8_LO = AT_TAB2 + 4 * T
AT_STAGED = AT_W8_LO + 9 * H
AT_W8_HI = AT_STAGED + 4 * H
WOVEN = 2 * PACK * S
AT_H_FLAT = AT_W8_HI + 4 * H
AT_HQ = AT_H_FLAT + 2 * WOVEN
AT_SIG = AT_HQ + 2 * WOVEN
W4S = KP * H // 4
SW = S // 4


def tile_list_repository_matrix_kernel(
    tc, tab_words, tab_scales, offs, w4_words, w4_scales, w8_words, w8_scales, docs, b1, gain, b2, out
):
    nc = tc.nc
    with ExitStack() as ctx:
        keep = ctx.enter_context(tc.tile_pool(name="keep", bufs=1))
        shared = ctx.enter_context(tc.tile_pool(name="shared", bufs=1))
        psum = ctx.enter_context(tc.psum_pool(name="psum", bufs=1))

        def sb(shape, dtype, name, tag=None):
            return keep.tile(shape, dtype, name=name, tag=tag or name, align_bytes=256)

        def placed(shape, dtype, name, offset):
            return shared.tile(shape, dtype, name=name, tag=name, align_bytes=256, offset=offset)

        def bank(n, shape, name):
            return psum.tile(shape, F32, name=name, tag="bank%d" % n)

        offsets = keep.tile([P, S // 16], U16, name="offsets")
        nc.sync.dma_start(offsets[:], offs)

        w4_all = w4_words.bitcast(I32)
        w4_first = sb([P, H // 2], I32, "w4_first")
        nc.sync.dma_start(w4_first[:], w4_all[ORDER[0]])
        staged = placed([P, W4S + SW], I32, "staged", AT_STAGED)
        nc.sync.dma_start(
            staged[4:P:8, 0:W4S].rearrange("q (a n) -> q a n", a=KP),
            w4_scales.bitcast(I32).rearrange("a q n -> q a n"),
        )

        rows = sb([P, 32], F32, "rows")
        win_a = sb([P, T], U8, "win_a")
        win_b = sb([P, T], U8, "win_b")

        def clear(words):
            cut = words.shape[1] // 2 + 1
            nc.vector.memset(words[:, 0:cut], 0)
            nc.vector.memset(words[:, cut:], 0)

        nc.gpsimd.memset(rows[:], 0.0)
        nc.gpsimd.memset(win_a[:].bitcast(I32), 0)
        nc.vector.memset(win_b[:].bitcast(I32), 0)

        def load_vector(n, vec):
            nc.sync.dma_start(
                rows[n:P:4, :].rearrange("u (g i) -> u g i", i=RUN),
                vec.rearrange("(g u i) -> u g i", u=32, i=RUN),
            )

        load_vector(0, b1)
        load_vector(1, gain)
        tab_rows = tab_scales.bitcast(I32)
        nc.sync.dma_start(win_a[0:P:4, :].bitcast(I32), tab_rows[0:2].rearrange("a q n -> q a n"))
        nc.sync.dma_start(win_b[0:P:8, :].bitcast(I32), tab_rows[2])

        w8s_raw = sb([P, H // 4], I32, "w8s_raw")
        planes_first = sb([P, W4S + SW], I32, "planes_first")
        planes_later = sb([P, 2 * SW], I32, "planes_later")
        clear(w8s_raw[:])
        clear(planes_first[:])

        def load_tab(a, tab):
            nc.sync.dma_start(tab[:], tab_words[ORDER[a]].rearrange("p t i -> p (t i)").bitcast(I32))
            return tab

        tabs = [load_tab(0, placed([P, T], I32, "tab0", AT_W8_LO))]
        w4_later = placed([P, 2, H // 2], I32, "w4_later", AT_W8_HI)
        nc.sync.dma_start(w4_later[:], w4_all[0:KP:2].rearrange("a p n -> p a n"))
        load_vector(2, b2)
        for d in range(4):
            nc.gpsimd.dma_start(w8s_raw[32 * d + 4 : 32 * d + 4 * (KP + 1), :], w8_scales.bitcast(I32)[:, 4 * d : 4 * d + 4, :])

        pick_a = placed([P, S], U8, "pick_a", AT_TAB1)
        nc.vector.tensor_copy(pick_a[:], win_a[:].indirect(offsets[:]))
        nc.vector.tensor_copy(staged[:, W4S : W4S + SW], pick_a[:].bitcast(I32))
        nc.vector.tensor_copy(planes_later[:, 0:SW], pick_a[:].bitcast(I32))
        for r in range(4):
            nc.sync.dma_start(planes_first[r:P:32, :], staged[8 * r + 4 : P : 32, :])
        tabs.append(load_tab(1, placed([P, T], I32, "tab1", AT_TAB1)))
        pick_b = placed([P, S], U8, "pick_b", AT_TAB2)
        nc.vector.tensor_copy(pick_b[:], win_b[:].indirect(offsets[:]))
        nc.vector.tensor_copy(planes_later[:, SW : 2 * SW], pick_b[:].bitcast(I32))
        for r in range(1, 4):
            nc.sync.dma_start(planes_later[r:P:32, :], planes_later[8 * r : P : 32, :])
        tabs.append(load_tab(2, placed([P, T], I32, "tab2", AT_TAB2)))

        def permute(dst, src, words, tiles=slice(0, CT)):
            nc.vector.tensor_copy(
                dst.rearrange("p (c q g w) -> p c q g w", q=4, g=4, w=words),
                src.rearrange("p (g q c w) -> p c q g w", c=CT, q=4, w=words)[:, tiles],
            )

        def gather_words(a):
            v = sb([P, S], I32, "v%d" % a)
            nc.vector.tensor_copy(v[:].bitcast(U32), tabs[a][:].bitcast(U32).indirect(offsets[:]))
            return v

        w4 = []
        w4s = []

        def order_w4(a):
            if a == 0:
                w = sb([P, H // 2], I32, "w4_0")
            else:
                w = placed([P, H // 2], I32, "w4_%d" % a, AT_STAGED + (a - 1) * 2 * H)
            permute(w[:], w4_first[:] if a == 0 else w4_later[:, a - 1, :], 4)
            w4.append(w)

        def order_w4_scales(a):
            ws = sb([P, H // 4], I32, "w4s_%d" % a)
            permute(ws[:], planes_first[:, ORDER[a] * H // 4 : (ORDER[a] + 1) * H // 4], 2)
            w4s.append(ws)

        order_w4(0)
        vs = [gather_words(0)]
        order_w4_scales(0)
        order_w4_scales(1)
        order_w4_scales(2)
        order_w4(1)
        order_w4(2)

        w8_all = w8_words.rearrange("a p n i -> p a (n i)").bitcast(I32)
        w8_raw = []
        for a, at in enumerate((AT_W8_LO, AT_W8_LO + 4 * H, AT_W8_HI)):
            w8_raw.append(placed([P, H], I32, "w8_raw%d" % a, at))
            nc.sync.dma_start(w8_raw[a][:], w8_all[:, ORDER[a], :])
        vs.append(gather_words(1))
        vs.append(gather_words(2))

        def w4_plane(a, c):
            return w4s[a][:].bitcast(U8)[:, c * P : (c + 1) * P]

        vecs = sb([P, CT, 4], F32, "vecs")
        nc.vector.transpose(vecs[:].rearrange("p c v -> p (c v)"), rows[:])

        bias = sb([P, RP, PACK], F32, "bias")
        bias_last = [placed([P, PACK], F32, "bias_last%d" % k, AT_HQ + k * 8 * S) for k in range(RP)]
        nc.vector.tensor_copy(bias[:].rearrange("p k t -> p (k t)"), vecs[:, :, 2])
        for k in range(RP):
            nc.vector.tensor_copy(bias_last[k][:], vecs[:, PACK * k : PACK * (k + 1), 2])

        def load_docs(a, raw):
            nc.sync.dma_start(raw[:], docs[512 * ORDER[a] : 512 * (ORDER[a] + 1), :].rearrange("(p j) w -> p j w", j=PACK))
            return raw

        docs_raw = [load_docs(0, placed([P, PACK, S], F32, "docs0", AT_DOCS0))]

        def v_scale(a, cols):
            if a == 0:
                return planes_first[:, W4S : W4S + SW].bitcast(U8)[:, cols]
            return planes_later[:].bitcast(U8)[:, (a - 1) * S + cols.start : (a - 1) * S + cols.stop]

        everything = slice(0, S)

        def a_pass(acc, c, a, stop):
            nc.tensor.matmul_mx(
                acc[:],
                lhsT=w4[a][:, c * 64 : (c + 1) * 64].bitcast(FP4X4),
                lhsT_scale=w4_plane(a, c),
                rhs=vs[a][:].bitcast(FP8X4),
                rhs_scale=v_scale(a, everything),
                start=(a == 0),
                stop=stop,
            )

        sig = [placed([P, PACK, S], F32, "sig0", AT_SIG), sb([P, PACK, S], F32, "sig1")]
        accs = [bank(c, [P, S], "a%d" % c) for c in range(CT)]
        for c in range(CT):
            a_pass(accs[c], c, 0, False)
        for c in range(CT):
            later = (1, 2) if c < EARLY else (2, 1)
            for a in later:
                a_pass(accs[c], c, a, a == later[-1])
            nc.scalar.activation(sig[c // PACK][:, c % PACK, :], accs[c][:], SIGMOID, bias=vecs[:, c, 0:1])

        def weave(copy, woven, flat, run):
            copy(woven.rearrange("p (n i) t -> p n t i", i=run), flat.rearrange("p t (n i) -> p n t i", i=run))

        def pool_cast(woven, raw):
            nc.gpsimd.tensor_scalar(woven, raw.rearrange("p t n -> p n t"), 1.0, 0.0, MULT, ADD)

        def quantized(name, at=None):
            codes = sb([P, S], I32, name + "_codes") if at is None else placed([P, S], I32, name + "_codes", at)
            return codes, sb([P, S], U8, name + "_plane")

        def quantize(dst, woven, cols=everything):
            nc.vector.quantize_mx(
                dst[0][:, cols].bitcast(FP8X4), dst[1][:, cols], woven[:, cols, :].rearrange("p n t -> p (n t)")
            )

        h_flat = [placed([P, PACK, S], BF16, "h_flat0", AT_H_FLAT + WOVEN // 2)]
        h_first = sb([P, S, PACK], BF16, "h_first")
        b_woven = []
        w8 = [sb([P, H], I32, "w8_%d" % a) for a in range(KP)]
        w8s = placed([P, H // 4], I32, "w8s", AT_TAB1)
        permute(w8s[:], w8s_raw[:], 2)
        permute(w8[0][:], w8_raw[0][:], 8)
        permute(w8[1][:], w8_raw[1][:], 8)
        permute(w8[2][:], w8_raw[2][:], 8)
        docs_raw.append(load_docs(1, placed([P, PACK, S], F32, "docs1", AT_TAB2)))
        docs_raw.append(load_docs(2, placed([P, PACK, S], F32, "docs2", AT_W8_LO + H)))
        for t in range(PACK):
            nc.vector.tensor_scalar_mul(h_flat[0][:, t, :], sig[0][:, t, :], vecs[:, t, 1:2])
        weave(nc.vector.tensor_copy, h_first[:], h_flat[0][:], 4)

        def b_pass(acc, c, a, n, start, stop):
            cols = slice(n * P, (n + 1) * P)
            nc.tensor.matmul_mx(
                acc,
                lhsT=w8[a][:, c * P : (c + 1) * P].bitcast(FP8X4),
                lhsT_scale=w8s[:].bitcast(U8)[4 * (ORDER[a] + 1) : P, c * P : (c + 1) * P],
                rhs=vs[a][:, cols].bitcast(FP8X4),
                rhs_scale=v_scale(a, cols),
                start=start,
                stop=stop,
            )

        def b_sums(k, order):
            sums = [bank(PACK * k + n, [P, PACK, P], "b%d_%d" % (k, n)) for n in range(MT)]
            for a, n in order:
                for t in range(PACK):
                    b_pass(sums[n][:, t, :], PACK * k + t, a, n, (a, t) == (0, 0), (a, t) == (KP - 1, PACK - 1))
            return sums

        def b_reads(k, sums):
            b_woven.append(placed([P, S, PACK], BF16, "b_woven%d" % k, AT_SIG + (3 - k) * WOVEN // 2))
            for n in range(MT):
                row = bias_last[k][:] if n == MT - 2 else bias[:, k, :]
                nc.vector.tensor_tensor(
                    b_woven[k][:, n * P : (n + 1) * P, :],
                    sums[n][:].rearrange("p t n -> p n t"),
                    row.unsqueeze(1).to_broadcast([P, P, PACK]),
                    ADD,
                )

        pool_part, scalar_part = slice(0, POOL_COLS), slice(POOL_COLS, S)
        bq = [quantized("b%d" % k) for k in range(RP)]

        sums = b_sums(0, [(a, n) for n in range(MT) for a in range(KP)])
        h_flat.append(placed([P, PACK, S], BF16, "h_flat1", AT_H_FLAT))
        for t in range(POOL_GAINS):
            nc.gpsimd.tensor_scalar(h_flat[1][:, t, :], sig[1][:, t, :], vecs[:, PACK + t, 1:2], 0.0, MULT, ADD)
        b_reads(0, sums)
        for t in range(POOL_GAINS, PACK):
            nc.scalar.activation(h_flat[1][:, t, :], sig[1][:, t, :], COPY, scale=vecs[:, PACK + t, 1:2])
        d_first = placed([P, S, PACK], BF16, "d_first", AT_SIG + 5 * WOVEN // 2)
        weave(nc.scalar.copy, d_first[:], docs_raw[0][:], 2)
        halves = [slice(0, S // 2), slice(S // 2, S)]
        d_woven = {a: sb([P, S, PACK], BF16, "d_woven%d" % a) for a in range(1, KP)}
        weave(nc.scalar.copy, d_woven[1][:], docs_raw[1][:], 2)
        sums = b_sums(1, [(a, n) for n in range(MT) for a in range(KP)])
        first_codes = placed([P, 2 * S], I32, "first_codes", AT_HQ)
        hq = [(first_codes[:, 0:S], sb([P, S], U8, "h0_plane")), quantized("h1")]
        dq = [(first_codes[:, S : 2 * S], sb([P, S], U8, "d0_plane"))]
        quantize(hq[0], h_first)
        quantize(bq[0], b_woven[0])
        quantize(dq[0], d_first)
        h_woven = placed([P, S, PACK], BF16, "h_woven", AT_SIG + 2 * WOVEN)
        pool_cast(h_woven[:, pool_part, :], h_flat[1][:, :, pool_part])
        b_reads(1, sums)
        weave(nc.scalar.copy, h_woven[:, scalar_part, :], h_flat[1][:, :, scalar_part], 4)
        for cols in halves:
            weave(nc.scalar.copy, d_woven[2][:, cols, :], docs_raw[2][:, :, cols], 2)
        d_codes = placed([P, 2 * S], I32, "d_codes", AT_HQ + 8 * S)
        dq.extend((d_codes[:, (a - 1) * S : a * S], sb([P, S], U8, "d%d_plane" % a)) for a in range(1, KP))
        for a in range(1, KP):
            quantize(dq[a], d_woven[a], halves[0])
        quantize(bq[1], b_woven[1])
        quantize(hq[1], h_woven)
        for a in range(1, KP):
            quantize(dq[a], d_woven[a], halves[1])

        def last_pass(acc, m, left, right, right_scale, start, stop):
            cols = slice(m * P, (m + 1) * P)
            nc.tensor.matmul_mx(
                acc[:],
                lhsT=left[0][:, cols].bitcast(FP8X4),
                lhsT_scale=left[1][:, cols],
                rhs=right.bitcast(FP8X4),
                rhs_scale=right_scale,
                start=start,
                stop=stop,
            )

        def d_pass(m, a):
            last_pass(d_accs[m], m, dq[a], vs[a][:], v_scale(a, everything), a == 0, a == KP - 1)

        def e_pass(m, k):
            last_pass(e_accs[m], m, hq[k], bq[k][0][:], bq[k][1][:], k == 0, k == RP - 1)

        d_accs = [bank(m, [P, S], "d%d" % m) for m in range(MT)]
        e_accs = [bank(PACK + m, [P, S], "e%d" % m) for m in range(MT)]
        for m in range(MT):
            d_pass(m, 0)
        for m in range(MT):
            e_pass(m, 0)
        kept = [sb([P, S], F32, "kept%d" % m) for m in range(MT)]

        def finish(m, acc):
            cut = {0: P, MT - 1: S - P}.get(m)
            for cols in [everything] if cut is None else [slice(0, cut), slice(cut, S)]:
                res = sb([P, cols.stop - cols.start], F32, "res%d_%d" % (m, cols.start))
                nc.vector.tensor_tensor(res[:], acc[:, cols], kept[m][:, cols], MULT)
                nc.sync.dma_start(out[m * P : (m + 1) * P, cols], res[:])

        for m in range(MT // 2):
            for a in range(1, KP):
                d_pass(m, a)
            nc.scalar.copy(kept[m][:], d_accs[m][:])
        for m in range(MT):
            e_pass(m, 1)
            if m < MT // 2:
                finish(m, e_accs[m])
            else:
                nc.scalar.copy(kept[m][:], e_accs[m][:])
        for m in range(MT // 2, MT):
            for a in range(1, KP):
                d_pass(m, a)
            finish(m, d_accs[m])
